import numpy as np, ml_dtypes
CORES = [6,15,38,47]
N = 4
BF = ml_dtypes.bfloat16
S, M, CAP, L = 1024, 768, 352, 4
F = 16 // N
def tries(rng, same=False, few=False):
    kid = np.zeros((N, 8, M, 16), np.int32); words = {}; deep = {}
    tid = (rng.integers(1, 65536, (N, 8, M)) * (rng.random((N, 8, M)) < (0.0625 if few else 0.5))).astype(np.int32)
    for q in range(N):
        for g in range(8):
            no = [0, 1] + (2 + rng.permutation(M - 2)).tolist(); pl = rng.random(M).tolist(); cl = rng.integers(0, 16, M).tolist()
            k = kid[q, g]; w = {1: []}; up = []; m = 2; deep[q, g] = []
            for c in (q * F + rng.permutation(F)).tolist()[:1 if few else F]:
                p = 1
                for d in range(L):
                    e = c if d == 0 or same else cl[m]
                    k[no[p], e] = no[m]; w[m] = w[p] + [e]
                    if d < L - 1: up.append(m)
                    p = m; m += 1
                tid[q, g, no[p]] = rng.integers(1, 65536); deep[q, g].append(w[p])
            for m in range(m, M):
                p = up[int(pl[m] * len(up))]; e = cl[m]
                if k[no[p], e]: continue
                k[no[p], e] = no[m]; w[m] = w[p] + [e]
                if len(w[m]) < L: up.append(m)
            words[q, g] = [v for v in w.values() if v]
    tid[:, :, 0] = 0
    return kid.reshape(N, 8, 16 * M), tid, words, deep
def strings(rng, words):
    s = np.zeros((8, N * S), np.int64)
    for g in range(8):
        qs = rng.integers(0, N, N * S).tolist(); ms = rng.random(N * S).tolist(); a = []; i = 0
        while len(a) < N * S:
            v = words[qs[i], g]; a += v[int(ms[i] * len(v))]; i += 1
        s[g] = a[:N * S]
    return np.where(rng.random(s.shape) < 0.1, rng.integers(0, 16, s.shape), s)
def plant(rng, s, deep):
    keep = np.zeros(s.shape, bool)
    for r in range(N):
        for g in range(8):
            v = deep[int(rng.integers(0, N)), g]; j = (r * S + S - 1 - g % (L - 1) + np.arange(L)) % (N * S)
            s[g, j] = v[int(rng.integers(0, len(v)))]; keep[g, j] = True
    return keep
def fit(rng, s, keep, full=False):
    s = s.reshape(8, N, S).transpose(1, 0, 2).astype(np.int32); keep = keep.reshape(8, N, S).transpose(1, 0, 2)
    a, b = int(rng.integers(0, N)), int(rng.integers(0, 8))
    for r in range(N):
        for g in range(8):
            e = s[r, g]; own = e // F; have = np.bincount(own, minlength=N); low = np.bincount(own[keep[r, g]], minlength=N)
            o = rng.permutation(N); i = np.flatnonzero((o == a) if full and g == b else (o != r))[0]; o[[0, i]] = o[[i, 0]]
            want = low.copy() if full else np.minimum(have, CAP)
            if full or (r, g) == (a, b): want[o[0]] = CAP
            for q in np.roll(o, -1): want[q] = min(max(int(want[q]) + S - int(np.sum(want)), int(low[q])), CAP)
            sur = np.concatenate([rng.permutation(np.flatnonzero((own == q) & ~keep[r, g]))[:max(int(have[q] - want[q]), 0)] for q in range(N)])
            need = np.repeat(np.arange(N), np.maximum(want - have, 0))
            e[sur] = need * F + rng.integers(0, F, len(need))
    return np.ascontiguousarray(s)
def setup_inputs(rng):
    kid, tid, words, deep = tries(rng); s = strings(rng, words); keep = plant(rng, s, deep)
    return {"lett": fit(rng, s, keep), "kid": kid, "tid": tid}
def setup_inputs_full(rng):
    kid, tid, words, deep = tries(rng); s = strings(rng, words)
    lett = fit(rng, s, np.zeros(s.shape, bool), True)
    assert np.sum((lett // F)[..., None] == np.arange(N), axis=2).min(axis=0).max() == CAP
    return {"lett": lett, "kid": kid, "tid": tid}
def setup_inputs_runs(rng):
    kid, tid, words, deep = tries(rng, same=True)
    s = np.stack([np.repeat(rng.integers(0, 16, N * S), rng.integers(1, 13, N * S))[:N * S] for g in range(8)]); keep = plant(rng, s, deep)
    return {"lett": fit(rng, s, keep), "kid": kid, "tid": tid}
def setup_inputs_few(rng):
    kid, tid, words, deep = tries(rng, few=True); s = strings(rng, words); keep = plant(rng, s, deep)
    return {"lett": fit(rng, s, keep), "kid": kid, "tid": tid}
def setup_inputs_spread(rng):
    kid = (rng.integers(0, M, (N, 8, M, 16)) * (rng.random((N, 8, M, 16)) > 0.125)).astype(np.int32)
    kid[:, :, 0] = 0; kid[:, :, 1] *= (np.arange(16) // F == np.arange(N)[:, None])[:, None, :]
    tid = (rng.integers(0, 65536, (N, 8, M)) * (rng.random((N, 8, M)) < 0.3)).astype(np.int32); tid[:, :, 0] = 0; tid[:, :, M - 1] = 65535
    s = np.minimum(np.floor(rng.random((8, N * S)) ** 2 * 16), 15).astype(np.int64)
    return {"lett": fit(rng, s, np.zeros(s.shape, bool)), "kid": kid.reshape(N, 8, 16 * M), "tid": tid}
def check_inputs(d):
    bad = []; s, kid, tid = d["lett"], d["kid"], d["tid"]
    if s.min() < 0 or s.max() > 15: bad.append("letters")
    if ((s // F)[..., None] == np.arange(N)).sum(2).max() > CAP: bad.append("slots")
    if kid.min() < 0 or kid.max() >= M: bad.append("children")
    if kid[:, :, :16].any() or tid[:, :, 0].any(): bad.append("node 0")
    if (kid[:, :, 16:32] * (np.arange(16) // F != np.arange(N)[:, None])[:, None, :]).any(): bad.append("roots")
    if tid.min() < 0 or tid.max() > 65535: bad.append("ids")
    return bad
def reference(lett, kid, tid):
    s = np.concatenate(list(lett), axis=1).astype(np.int64)
    own = s // F; g = np.arange(8)[:, None]; node = np.ones(s.shape, np.int64); yl = np.zeros(s.shape, np.int64); yi = np.zeros(s.shape, np.int64)
    for k in range(L):
        node = kid[own, g, 16 * node + np.roll(s, -k, axis=1)].astype(np.int64)
        t = tid[own, g, node]
        yl = np.where(t > 0, k + 1, yl); yi = np.where(t > 0, t, yi)
    yl = np.ascontiguousarray(yl.reshape(8, N, S).transpose(1, 0, 2)); yi = np.ascontiguousarray(yi.reshape(8, N, S).transpose(1, 0, 2))
    return {"ylen": yl.astype(np.float32), "yid": yi.astype(np.float32)}

@@ -1,0 +1,480 @@
+import numpy as np
+from concourse.bass import DstId, RemoteDMATransfer
+from concourse.mybir import AluOpType as A, ActivationFunctionType as F
+
+NR = 4
+M = 768
+OFF = 1536.0
+SA, SF, SN, SM = 320, 256, 256, 352
+CUT = 480
+IV = 832
+K17 = 131072.0
+RND = 12582912.0 * K17
+HF = "float16"
+BF = "bfloat16"
+F32 = "float32"
+I32 = "int32"
+U16 = "uint16"
+
+
+def sb(cols, dtype):
+    return ("sbuf", [128] + (cols if isinstance(cols, list) else [cols]), dtype)
+
+
+SCRATCH = {
+    "lbuf": ("dram", [4, 128, 16], HF), "lin": ("dram", [4, 128, 16], HF),
+    "tbuf": ("dram", [4, 128, 12], I32), "tin": ("dram", [4, 128, 12], I32),
+    "lx": sb(64, I32), "lf": sb(64, HF), "kx": sb([12, 64], I32), "kh": sb([6, 128], HF),
+    "ks": sb(768, HF), "kin": sb(768, HF),
+    "win": sb(3072, F32), "tw": sb(3072, BF), "nw": sb(256, F32),
+    "ht": sb(192, I32), "hb": sb(576, BF),
+    "lu": sb(1040, HF), "ll": sb(136, HF), "em": sb(1072, BF),
+    "pi": sb(1, I32), "pci": sb(1, I32),
+    "pcf": sb(1, F32), "k16": sb(1, F32), "zz": sb(1, F32), "sa": sb(1, F32), "sk": sb(1, F32),
+    "imk": sb(143, BF), "frk": sb(128, BF), "e8i": sb(128, BF), "pdi": sb(128, BF), "one": sb(128, BF),
+    "expi": sb(16, I32), "expu": sb(16, U16),
+    "e8": sb(128, HF), "ih": sb(128, HF), "i16": sb(128, HF), "sh1": sb(128, HF),
+    "r0": sb(128, HF), "r1": sb(128, HF), "r2": sb(128, HF), "r3": sb(128, HF),
+    "id": sb(128, F32), "ib": sb(128, BF), "shb": sb(128, BF), "t1h": sb(143, HF), "vt": sb(32, BF),
+    "cu": sb(64, U16), "n1u": sb(8, U16), "n2u": sb(64, U16), "n3u": sb(64, U16), "n4u": sb(64, U16),
+    "p3": sb(1024, HF), "p4": sb(1024, HF),
+    "g1": sb(64, BF), "g1e": sb(256, BF), "g2": sb(256, BF), "g12": sb(256, BF),
+    "i12": sb(1024, BF), "i3": sb(1024, BF), "i4": sb(1024, BF),
+    "b1": sb(64, F32), "b2": sb(64, F32), "b3": sb(64, F32),
+    "res": sb(64, F32), "rcv": sb(64, F32), "rt": sb(128, F32), "yl": sb(128, F32), "yi": sb(128, F32),
+}
+for _i in range(8):
+    SCRATCH["ps%d" % _i] = ("psum", [128, 512], F32)
+SEMAPHORES = (["cv", "ca", "ct", "cg", "sl", "st", "sr"]
+              + ["%s%d" % (x, i) for x in ("sk", "rl", "rt", "rk", "rr") for i in range(NR)] + ["d%d" % i for i in range(48)])
+
+
+def shares(topo, src, dsts):
+    far = [d for d in dsts if not topo.mates(topo.chip(src), topo.chip(d))
+           and not topo.same_plane(topo.chip(src), topo.chip(d))]
+    order = far + [d for d in dsts if d not in far]
+    out = {}
+    at = 0
+    for i, d in enumerate(order):
+        e = topo.engines(src, d)
+        n = len(e) // 2 if i == 0 else len(e) // 4
+        out[d] = e[at:at + n]
+        at += n
+    return out
+
+
+def bits(engines):
+    return sum(1 << e for e in engines)
+
+
+def rank_program(g, core, T, topo):
+    me = T.rank_of(core)
+    if me is None:
+        return
+    cores = list(T.cores)
+    others = [q for q in range(NR) if q != me]
+    mate = [q for q in others if topo.mates(topo.chip(core), topo.chip(cores[q]))]
+    plane = [q for q in others if topo.same_plane(topo.chip(core), topo.chip(cores[q]))]
+    order = [q for q in others if q not in mate + plane] + plane + mate
+    f, n, m = order
+    q_of = {"g": g, "v": g.vector, "a": g.scalar, "t": g.tensor, "s": g.sync}
+    csem = {"g": "cg", "v": "cv", "a": "ca", "t": "ct"}
+    total = {}
+    waited = {}
+    seen = {}
+    lastw = {}
+    reads = {}
+    ndma = [0]
+
+    def wait(q, evs):
+        most = {}
+        for s, x in evs:
+            most[s] = max(x, most.get(s, 0))
+        for s in most:
+            if waited.get((q, s), 0) < most[s]:
+                q_of[q].wait_ge(T.sem[s], most[s])
+                waited[(q, s)] = most[s]
+                seen[s] = max(seen.get(s, 0), most[s])
+
+    def deps(q, R, W):
+        own = csem.get(q)
+        evs = []
+        for k in R:
+            evs += lastw.get(k, [])
+        for k in W:
+            evs += [e for e in lastw.get(k, []) + reads.get(k, []) if e[0] != own]
+        wait(q, evs)
+
+    def note(ev, R, W):
+        for k in W:
+            lastw[k] = [ev]
+            reads[k] = []
+        for k in R:
+            reads.setdefault(k, []).append(ev)
+
+    def comp(q, R, W, calls):
+        deps(q, R, W)
+        s = csem[q]
+        for c in (calls if isinstance(calls, list) else [calls]):
+            c().then_inc(T.sem[s], 1)
+            total[s] = total.get(s, 0) + 1
+        note((s, total[s]), R, W)
+
+    def V(R, W, *calls):
+        comp("v", R, W, list(calls))
+
+    def act(R, W, o, i):
+        comp("a", R, W, lambda: g.scalar.activation(o, i, F.Copy))
+
+    def dma(q, out, in_, R, W):
+        deps(q, R, W)
+        s = "d%d" % ndma[0]
+        ndma[0] += 1
+        q_of[q].dma_start(out, in_).then_inc(T.sem[s], 16)
+        total[s] = 16
+        note((s, 16), R, W)
+
+    def arrive(s, x, keys):
+        total[s] = total.get(s, 0) + x
+        for k in keys:
+            lastw[k] = [(s, total[s])]
+
+    def dst(d):
+        rid, pid, _ = topo.addr(d)
+        return DstId(rid=rid, pnc=pid)
+
+    mine = shares(topo, core, [cores[q] for q in others])
+
+    def send(rsem, lsem, way, src_of, out, R):
+        deps("g", R, [])
+        tr = [RemoteDMATransfer(dst_ids=[dst(cores[q])], dma_engine_mask=bits(e), remote_sem=T.sem["%s%d" % (rsem, me)],
+                                src=src_of(q), dst=out) for q, e in way]
+        g.remote_dma_fused(tr, local_sem=T.sem[lsem])
+        total[lsem] = total.get(lsem, 0) + sum(len(e) for q, e in way)
+
+    def got(q):
+        return len(shares(topo, cores[q], [c for c in cores if c != cores[q]])[core])
+
+    v = g.vector
+    pe = g.tensor
+    ps = [T["ps%d" % i] for i in range(8)]
+
+    def load(q):
+        p = slice(32 * q, 32 * q + 32)
+        dma("s", T.kx[p, 0:6, :], T.kid[2 * q, :], [], ["kx0_%d" % q])
+        dma("a", T.kx[p, 6:12, :], T.kid[2 * q + 1, :], [], ["kx1_%d" % q])
+
+    dma("a", T.lx[:], T.lett[:], [], ["lx"])
+    load(f)
+    dma("s", T.tbuf[:], T.tid[:], [], ["tbuf"])
+    for q in (n, m, me):
+        load(q)
+    dma("s", T.tin[me], T.tid[2 * me:2 * me + 2, :], [], ["tin%d" % me])
+
+    def iota(key, out, pattern, base, mult):
+        comp("g", [], [key], lambda: g.iota(out, pattern, base, mult, allow_small_or_imprecise_dtypes=True))
+
+    comp("g", [], ["pi"], lambda: g.iota(T.pi[:], [[1, 1]], 0, 1))
+    iota("imk", T.imk[:], [[1, 143]], 0, -1)
+    iota("frk", T.frk[:], [[0, 4], [64, 2], [1, 16]], 0, -1)
+    comp("g", [], ["expi"], lambda: g.iota(T.expi[:], [[20, 4], [1, 4]], 0, 0))
+    send("rt", "st", [(q, mine[cores[q]]) for q in others], lambda q: T.tbuf[q], T.tin[me], ["tbuf"])
+
+    V([], ["tz0"], lambda: v.memset(T.tw[:, 0:512], 0.0))
+    act(["tz0"], ["tz1"], T.tw[:, 512:1024], T.tw[:, 0:512])
+    V(["pi"], ["pci"], lambda: v.tensor_scalar(T.pci[:], T.pi[:], 15, None, A.bitwise_and))
+    V(["pi"], ["sa"], lambda: v.tensor_scalar(T.sa[:], T.pi[:], 32.0, 128.0, A.is_lt, A.mult))
+    V(["pci"], ["pcf"], lambda: v.tensor_copy(T.pcf[:], T.pci[:]))
+    V(["imk"], ["ih"], lambda: v.tensor_scalar(T.ih[:], T.imk[:, 0:128], 0.0, None, A.is_equal))
+    V(["pcf"], ["zz"], lambda: v.tensor_scalar(T.zz[:], T.pcf[:], 0.0, None, A.is_equal))
+    V(["pcf"], ["k16"], lambda: v.tensor_scalar(T.k16[:], T.pcf[:], -1.0, 15.0, A.mult, A.add))
+    V(["sa", "zz"], ["sk"], lambda: v.tensor_scalar(T.sk[:], T.sa[:], -16.0, T.zz[:], A.add, A.mult))
+    act(["lx"], ["lf"], T.lf[:], T.lx[:])
+    dma("s", T.lbuf[:], T.lf[:], ["lf"], ["lbuf"])
+    dma("s", T.lin[me], T.lf[32 * me:32 * me + 32, :], ["lf"], ["lin%d" % me])
+    tz = ["tz%d" % x for x in range(6)]
+
+    code = float(M * me) - OFF
+    eng = topo.engines(core, cores[f])
+
+    def cast(q):
+        p = slice(32 * q, 32 * q + 32)
+        V(["kx0_%d" % q], ["kh0_%d" % q], lambda: v.tensor_copy(T.kh[p, :, 0:64], T.kx[p, 0:6, :]))
+        act(["kx1_%d" % q], ["kh1_%d" % q], T.kh[p, :, 64:128], T.kx[p, 6:12, :])
+
+    def turn(q):
+        p = slice(32 * q, 32 * q + 32)
+        comp("t", ["kh0_%d" % q, "kh1_%d" % q, "ih"], ["ps%d" % q],
+             [lambda b=b: pe.matmul(ps[q][:, b:192:6], T.kh[p, b, :], T.ih[p, p], True, True) for b in range(6)])
+
+    def leave(q, by):
+        o, i = T.ks[:, 192 * q:192 * q + 192], ps[q][:, 0:192]
+        if by == "v":
+            V(["ps%d" % q], ["ks%d" % q], lambda: v.tensor_scalar(o, i, code, None, A.add))
+        else:
+            comp("a", ["ps%d" % q], ["ks%d" % q], lambda: g.scalar.activation(o, i, F.Copy, bias=code))
+
+    def go(q):
+        send("rk", "sk%d" % q, [(q, eng)], lambda d: T.ks[:, 192 * d:192 * d + 192], T.kin[:, 192 * me:192 * me + 192],
+             ["ks%d" % q])
+
+    cast(f)
+    turn(f)
+    cast(n)
+    leave(f, "v")
+    go(f)
+    send("rl", "sl", [(d, mine[cores[d]]) for d in others], lambda d: T.lbuf[d], T.lin[me], ["lbuf"])
+    turn(n)
+    cast(m)
+    turn(m)
+    leave(n, "a")
+    go(n)
+    cast(me)
+    turn(me)
+    leave(m, "v")
+    go(m)
+    leave(me, "a")
+    act(["tz0"], ["tz3"], T.tw[:, 1536:2048], T.tw[:, 0:512])
+    for q in others:
+        arrive("rl%d" % q, got(q), ["lin%d" % q])
+        arrive("rt%d" % q, got(q), ["tin%d" % q])
+        arrive("rk%d" % q, len(eng), ["kin%d" % q])
+
+    iota("e8i", T.e8i[0:8, :], [[1, 8], [0, 16]], 0, -1)
+    iota("tz5", T.tw[:, 2304:3072], [[0, 768]], 0, 0)
+    iota("one", T.one[:], [[0, 128]], 1, 0)
+    comp("g", ["one"], ["ib"], lambda: g.affine_select(T.ib[:], T.one[:], [[1, 128]], A.is_equal, 0.0, 0, -1))
+    comp("g", ["one"], ["shb"], lambda: g.affine_select(T.shb[:], T.one[:], [[1, 128]], A.is_equal, 0.0, -3, -1))
+    iota("vt", T.vt[:], [[0, 32]], 0, 0)
+
+    def weight(j, k, x, w):
+        i = T.vt[:, 8 * j:8 * k]
+        comp("g", ["vt"], ["vt"], lambda: g.affine_select(i, i, [[0, k - j], [-16, 8]], A.not_equal, w, -x, 1))
+
+    for x in range(2):
+        weight(0, 1, 3 + x, 1.0)
+        weight(1, 4, x, 1.0)
+    weight(0, 1, 5, K17)
+    for j in range(1, 4):
+        weight(j, j + 1, 2, (j + 1) * K17)
+    iota("pdi", T.pdi[:], [[1, 2], [2, 64]], 0, -1)
+
+    lins = ["lin%d" % q for q in range(4)]
+    tins = ["tin%d" % q for q in range(4)]
+    for x in range(4):
+        dma("s", T.ht[16 * x:16 * x + 16, :], T.tin[:, 64 * (x % 2):64 * (x % 2) + 64, :], tins, ["ht%d" % x])
+    dma("s", T.lu[0:8, 0:1024], T.lin[:], lins, ["lua"])
+    dma("s", T.lu[0:6, 1024:1040], T.lin[1:4, 0::64, :], lins, ["lub"])
+    dma("s", T.lu[6:8, 1024:1040], T.lin[0, 0::64, :], lins, ["luc"])
+    lus = ["lua", "lub", "luc"]
+
+    def sums(q, ka, kb, va):
+        src, keys = (T.ks, ["ks%d" % me]) if q == me else (T.kin, ["kin%d" % q])
+        c = 192 * q
+        for k, a, b in ((ka, 0, va // 4), (kb, va // 4, 192)):
+            comp("t", keys + ["r%d" % x for x in range(4)], ["ps%d" % k],
+                 [lambda x=x: pe.matmul(ps[k][:, x:4 * (b - a):4], T["r%d" % x][:], src[:, c + a:c + b], True, True)
+                  for x in range(4)])
+
+    def copyv(q, ka, va):
+        V(["ps%d" % ka], ["wa%d" % q], lambda: v.tensor_copy(T.win[:, M * q:M * q + va], ps[ka][:, 0:va]))
+
+    def copya(q, kb, va):
+        act(["ps%d" % kb], ["wb%d" % q], T.win[:, M * q + va:M * q + M], ps[kb][:, 0:M - va])
+
+    def block(q):
+        return T.win[:, M * q:M * q + M], T.tw[:, M * q:M * q + M], OFF - M * q
+
+    def table1(q):
+        V(["wa%d" % q], ["n1_%d" % q],
+          lambda: v.tensor_scalar(T.n1u[:, 2 * q:2 * q + 1], T.win[:, M * q + 1:M * q + 2], block(q)[2], None, A.add))
+
+    def table2(q, by="v"):
+        R, o, i = ["wa%d" % q, "wb%d" % q, "n1_%d" % q], T.n2u[:, 16 * q:16 * q + 16], T.n1u[:, 2 * q:2 * q + 1]
+        if by == "v":
+            V(R, ["n2_%d" % q], lambda: v.tensor_scalar(o, block(q)[0].indirect(i), block(q)[2], None, A.add))
+        else:
+            comp("a", R, ["n2_%d" % q], lambda: g.scalar.activation(o, block(q)[0].indirect(i), F.Copy, bias=block(q)[2]))
+
+    def table3(q, by="v"):
+        R, o, i = ["wa%d" % q, "wb%d" % q, "n2_%d" % q], T.nw[:, 64 * q:64 * q + 64], T.n2u[:, 20 * q:20 * q + 4]
+        if by == "v":
+            V(R, ["nw%d" % q], lambda: v.tensor_copy(o, block(q)[0].indirect(i)))
+        else:
+            act(R, ["nw%d" % q], o, block(q)[0].indirect(i))
+
+    tws = []
+
+    def idlists(q):
+        act(tws + ["n1_%d" % q], ["g1_%d" % q], T.g1[:, 16 * q:16 * q + 16], block(q)[1].indirect(T.n1u[:, 2 * q:2 * q + 1]))
+        act(tws + ["n2_%d" % q], ["g2_%d" % q], T.g2[:, 64 * q:64 * q + 64],
+            block(q)[1].indirect(T.n2u[:, 20 * q:20 * q + 4]))
+
+    for x in range(4):
+        V(["frk"], ["r%d" % x], lambda: v.tensor_scalar(T["r%d" % x][:], T.frk[:], float(-16 * x), None, A.is_equal))
+    sums(me, 4, 5, SA)
+    V(["expi"], ["expu"], lambda: v.tensor_copy(T.expu[:], T.expi[:]))
+    V(["imk"], ["llz"], lambda: v.tensor_scalar(T.ll[:], T.imk[:, 0:136], 0.0, None, A.mult))
+    V([], ["tz2"], lambda: v.memset(T.tw[:, 1024:1536], 0.0))
+    copyv(me, 4, SA)
+    copya(me, 5, SA)
+    comp("a", ["ih"], ["i16"], lambda: g.scalar.activation(T.i16[:], T.ih[:], F.Copy, scale=16.0))
+    V(["imk", "sk"], ["sh1"], lambda: v.tensor_scalar(T.sh1[:], T.imk[:, 0:128], 1.0, T.sk[:], A.add, A.is_equal))
+    V(["imk", "k16"], ["t1h"], lambda: v.tensor_scalar(T.t1h[:], T.imk[:], T.k16[:], None, A.is_equal))
+    deps("s", ["llz"], [])
+    dma("s", T.ll[:, 64:128], T.lin[:], lins, ["ll"])
+    table1(me)
+    table2(me)
+    table3(me)
+    V([], ["tz4"], lambda: v.memset(T.tw[:, 2048:2304], 0.0))
+    V(["e8i"], ["e8"], lambda: v.tensor_scalar(T.e8[0:8, :], T.e8i[0:8, :], 0.0, None, A.is_equal))
+
+    sums(f, 6, 7, SF)
+    copyv(f, 6, SF)
+    copya(f, 7, SF)
+    table1(f)
+
+    hts = ["ht%d" % x for x in range(4)]
+    act(hts, ["hb0"], T.hb[0:64, 0:192], T.ht[0:64, :])
+    comp("a", hts, ["hb2"], lambda: g.scalar.activation(T.hb[0:64, 384:576], T.ht[0:64, :], F.Sign))
+    V(hts + ["hb0"], ["hb1"], lambda: v.tensor_tensor(T.hb[0:64, 192:384], T.ht[0:64, :], T.hb[0:64, 0:192], A.subtract))
+    for x in (0, 2, 1):
+        for s in range(2):
+            deps("s", tz, [])
+            dma("s", T.tw[64 * s + x:64 * s + 64:16, :], T.hb[0:64, 192 * x:192 * x + 192], ["hb%d" % x],
+                ["tw%d%d" % (x, s)])
+            tws.append("tw%d%d" % (x, s))
+
+    def letters(k):
+        comp("t", ["lua", "e8"], ["ps%d" % (2 + k)],
+             [lambda s=s: pe.matmul(ps[2 + k][:, s:512:8], T.e8[0:8, :], T.lu[0:8, 128 * s + 64 * k:128 * s + 64 * k + 64],
+                                    True, True) for s in range(8)])
+
+    def mask(k):
+        V(["ps%d" % (2 + k), "pcf"], ["em%d" % k],
+          lambda: v.tensor_scalar(T.em[:, k:1024:2], ps[2 + k][:, 0:512], T.pcf[:], None, A.is_equal))
+
+    def more():
+        comp("t", lus + ["e8"], ["ps0"],
+             [lambda e=e: pe.matmul(ps[0][:, 16 * e:16 * e + 16], T.e8[0:8, :], T.lu[0:8, 64 + e:64 + e + 961:64], True, True)
+              for e in range(3)])
+        comp("t", ["ll", "llz", "i16", "ih", "sh1"], ["ps1"],
+             [lambda: pe.matmul(ps[1][:, 0:64], T.i16[:], T.ll[:, 64:128], True, False),
+              lambda: pe.matmul(ps[1][:, 0:64], T.ih[:], T.ll[:, 65:129], False, False),
+              lambda: pe.matmul(ps[1][:, 0:64], T.sh1[:], T.ll[:, 1:65], False, True)])
+
+    ems = ["em0", "em1", "em2"]
+
+    sums(n, 4, 5, SN)
+    copyv(n, 4, SN)
+    copya(n, 5, SN)
+    letters(0)
+    letters(1)
+    more()
+    sums(m, 6, 7, SM)
+    table1(n)
+    mask(0)
+    table2(f, "a")
+    table3(f, "a")
+    mask(1)
+    act(["ps1"], ["cu"], T.cu[:], ps[1][:, 0:64])
+    V(["ps0", "pcf"], ["em2"], lambda: v.tensor_scalar(T.em[:, 1024:1072], ps[0][:, 0:48], T.pcf[:], None, A.is_equal))
+    copyv(m, 6, SM)
+    copya(m, 7, SM)
+    table2(n)
+    table1(m)
+    table3(n)
+    table2(m)
+    table3(m)
+    for q in (me, f, n, m):
+        idlists(q)
+    act(["g1_%d" % q for q in range(4)] + ["expu"], ["g1e"], T.g1e[:], T.g1[:, 0:64].indirect(T.expu[:, 0:16]))
+    wk = ["w%s%d" % (x, q) for q in range(4) for x in "ab"]
+    nws = ["nw%d" % q for q in range(4)]
+    g2s = ["g2_%d" % q for q in range(4)]
+    win = T.win[:, 0:3072]
+    twin = T.tw[:, 0:3072]
+
+    portions = ((0, CUT), (CUT, 1024))
+
+    def walk(p, h, w, lst, e, R):
+        a, b = portions[h]
+        V(R + ems, ["%s%d" % (p, h)],
+          lambda: v.tensor_tensor(T[p][:, a:b], w.indirect(lst[:, a // 16:b // 16]), T.em[:, a + 16 * e:b + 16 * e], A.mult))
+
+    def nodes(bank, p, h):
+        a, b = portions[h]
+        comp("t", ["%s%d" % (p, h), "t1h"], ["ps%d" % bank],
+             [lambda i=i: pe.matmul(ps[bank][:, 0:(b - a) // 16], T.t1h[:, 15 - i:143 - i], T[p][:, a + i:b:16], i == 0,
+                                    i == 15) for i in range(16)])
+
+    def lists(bank, nm, h):
+        a, b = portions[h]
+        V(["ps%d" % bank], ["%s%d" % (nm, h)],
+          lambda: v.tensor_scalar(T[nm][:, a // 16:b // 16], ps[bank][:, 0:(b - a) // 16], OFF, None, A.add))
+
+    pieces = {"i12": [], "i3": [], "i4": []}
+
+    def ids(q, rep, w, lst, a, b, R):
+        key = "%s_%d" % (rep, a)
+        pieces[rep].append(key)
+        i = w.indirect(lst[:, a // 16:b // 16])
+        if q == "v":
+            V(R, [key], lambda: v.tensor_copy(T[rep][:, a:b], i))
+        else:
+            act(R, [key], T[rep][:, a:b], i)
+
+    def value(rep, bank, x, j):
+        comp("t", pieces[rep] + ["vt"], ["ps%d" % bank],
+             [lambda s=s: pe.matmul(ps[bank][:, s:64 * x:8], T[rep][:, s:1024:8], T.vt[:, 8 * j:8 * j + 8 * x], True, True)
+              for s in range(8)])
+
+    walk("p3", 0, T.nw[:, 0:256], T.cu, 2, nws + ["cu"])
+    comp("t", ["g1e", "shb", "ib"] + g2s, ["ps0"],
+         [lambda: pe.matmul(ps[0][:, 0:256], T.shb[:], T.g1e[:], True, False),
+          lambda: pe.matmul(ps[0][:, 0:256], T.ib[:], T.g2[:], False, True)])
+    act(["ps0"], ["g12"], T.g12[:], ps[0][:, 0:256])
+    nodes(4, "p3", 0)
+    walk("p3", 1, T.nw[:, 0:256], T.cu, 2, nws + ["cu"])
+    nodes(5, "p3", 1)
+    for a in (0, 512):
+        ids("a", "i12", T.g12[:, 0:256], T.cu, a, a + 512, ["g12", "cu"])
+    for h in range(2):
+        lists(4 + h, "n3u", h)
+        walk("p4", h, win, T.n3u, 3, wk + ["n3u%d" % h])
+        nodes(6 + h, "p4", h)
+        ids("a", "i3", twin, T.n3u, portions[h][0], portions[h][1], tws + ["n3u%d" % h])
+    value("i12", 1, 2, 0)
+    value("i3", 3, 1, 2)
+    lists(6, "n4u", 0)
+    ids("v", "i4", twin, T.n4u, 0, CUT, tws + ["n4u0"])
+    lists(7, "n4u", 1)
+    ids("v", "i4", twin, T.n4u, CUT, IV, tws + ["n4u1"])
+    ids("a", "i4", twin, T.n4u, IV, 1024, tws + ["n4u1"])
+    V(["ps1"], ["b1"], lambda: v.tensor_copy(T.b1[:], ps[1][:, 64:128]))
+    V(["ps1", "b1"], ["b2"], lambda: v.tensor_tensor(T.b2[:], ps[1][:, 0:64], T.b1[:], A.max))
+    value("i4", 0, 1, 3)
+    V(["ps3", "b2"], ["b3"], lambda: v.tensor_tensor(T.b3[:], ps[3][:, 0:64], T.b2[:], A.max))
+    V(["ps0", "b3"], ["res"], lambda: v.tensor_tensor(T.res[:], ps[0][:, 0:64], T.b3[:], A.max))
+    V(["res"], ["rcv%d" % me],
+      lambda: v.tensor_copy(T.rcv[:, 16 * me:16 * me + 16], T.res[:, 16 * me:16 * me + 16]))
+    V(["pdi"], ["id"], lambda: v.tensor_scalar(T["id"][:], T.pdi[:], 0.0, None, A.is_equal))
+
+    half = len(eng) // 2
+    for way in ([(f, eng)], [(n, eng[:half]), (m, eng[half:])]):
+        send("rr", "sr", way, lambda d: T.res[:, 16 * d:16 * d + 16], T.rcv[:, 16 * me:16 * me + 16], ["res"])
+    for q in others:
+        arrive("rr%d" % q, len(eng) if q == f else half, ["rcv%d" % q])
+    p = ps[5][0:64, 0:128]
+    comp("t", ["rcv%d" % q for q in range(4)] + ["id"], ["ps5"],
+         lambda: pe.matmul(p, T.rcv[:], T["id"][:], True, True))
+    V(["ps5"], ["rt"], lambda: v.tensor_scalar(T.rt[0:64, :], p, RND, RND, A.add, A.subtract))
+    V(["ps5", "rt"], ["yi"], lambda: v.tensor_tensor(T.yi[0:64, :], p, T.rt[0:64, :], A.subtract))
+    comp("a", ["rt"], ["yl"], lambda: g.scalar.activation(T.yl[0:64, :], T.rt[0:64, :], F.Copy, scale=1.0 / K17))
+    for hi in range(2):
+        dma("s", T.yid[:, 512 * hi:512 * hi + 512], T.yi[0:64, 64 * hi:64 * hi + 64], ["yi"], ["oi%d" % hi])
+        dma("a", T.ylen[:, 512 * hi:512 * hi + 512], T.yl[0:64, 64 * hi:64 * hi + 64], ["yl"], ["ol%d" % hi])
+
+    for s in total:
+        if seen.get(s, 0) < total[s]:
+            wait("g", [(s, total[s])])

@@ -4,10 +4,10 @@ from concourse.mybir import AluOpType as A, ActivationFunctionType as F
 
 NR = 4
 M = 768
-OFF = 1536.0
-SA, SF, SN, SM = 320, 256, 256, 352
-CUT = 480
-IV = 832
+H = 384
+LO, HI = 128.0, 640.0
+CUT = 512
+IV = 800
 K17 = 131072.0
 RND = 12582912.0 * K17
 HF = "float16"
@@ -22,61 +22,92 @@ def sb(cols, dtype):
 
 
 SCRATCH = {
-    "lbuf": ("dram", [4, 128, 16], HF), "lin": ("dram", [4, 128, 16], HF),
-    "tbuf": ("dram", [4, 128, 12], I32), "tin": ("dram", [4, 128, 12], I32),
-    "lx": sb(64, I32), "lf": sb(64, HF), "kx": sb([12, 64], I32), "kh": sb([6, 128], HF),
-    "ks": sb(768, HF), "kin": sb(768, HF),
-    "win": sb(3072, F32), "tw": sb(3072, BF), "nw": sb(256, F32),
-    "ht": sb(192, I32), "hb": sb(576, BF),
-    "lu": sb(1040, HF), "ll": sb(136, HF), "em": sb(1072, BF),
-    "pi": sb(1, I32), "pci": sb(1, I32),
-    "pcf": sb(1, F32), "k16": sb(1, F32), "zz": sb(1, F32), "sa": sb(1, F32), "sk": sb(1, F32),
-    "imk": sb(143, BF), "frk": sb(128, BF), "e8i": sb(128, BF), "pdi": sb(128, BF), "one": sb(128, BF),
-    "expi": sb(16, I32), "expu": sb(16, U16),
-    "e8": sb(128, HF), "ih": sb(128, HF), "i16": sb(128, HF), "sh1": sb(128, HF),
-    "r0": sb(128, HF), "r1": sb(128, HF), "r2": sb(128, HF), "r3": sb(128, HF),
-    "id": sb(128, F32), "ib": sb(128, BF), "shb": sb(128, BF), "t1h": sb(143, HF), "vt": sb(32, BF),
-    "cu": sb(64, U16), "n1u": sb(8, U16), "n2u": sb(64, U16), "n3u": sb(64, U16), "n4u": sb(64, U16),
-    "p3": sb(1024, HF), "p4": sb(1024, HF),
-    "g1": sb(64, BF), "g1e": sb(256, BF), "g2": sb(256, BF), "g12": sb(256, BF),
+    "lx": sb(64, I32), "ht": sb(48, I32), "n1x": sb(1, I32), "hb": sb(208, BF), "hin": sb([4, 160], BF),
+    "kx": sb([2, 8, 48], I32), "kh": sb([2, 3, 128], HF), "kc": sb([2, 3, 128], HF),
+    "win": sb(3072, BF), "tw": sb(3072, BF), "nw": sb(256, BF), "g12": sb(256, BF),
+    "lu": sb(1024, BF), "sel": sb(128, BF), "em": sb(1072, BF),
+    "pi": sb(1, I32), "pci": sb(1, I32), "pcf": sb(1, F32), "k16": sb(1, F32), "zz": sb(1, F32), "nz": sb(1, F32),
+    "imk": sb(143, BF), "one": sb(128, BF), "onf": sb(128, F32),
+    "expi": sb(4, I32), "expu": sb(4, U16),
+    "e8": sb(128, BF), "ih": sb(128, HF), "ihn": sb(128, HF), "ib": sb(128, BF), "i16": sb(128, BF),
+    "sh": sb(128, BF), "sh15": sb(128, BF), "shb": sb(128, BF), "t1h": sb(143, BF), "vt": sb(32, BF), "id": sb(128, F32),
+    "ow": sb(64, I32), "off": sb(64, F32),
+    "cu": sb(64, U16), "n1u": sb(2, U16), "n2u": sb(16, U16), "n3u": sb(64, U16), "n4u": sb(64, U16),
+    "c2": sb(16, F32), "s2": sb(16, F32), "lc": sb(128, F32), "ls": sb(128, F32),
+    "p3": sb(1024, BF), "p4": sb(1024, BF),
+    "g1": sb(16, BF), "g1e": sb(64, BF), "g1s": sb(64, BF),
     "i12": sb(1024, BF), "i3": sb(1024, BF), "i4": sb(1024, BF),
     "b1": sb(64, F32), "b2": sb(64, F32), "b3": sb(64, F32),
-    "res": sb(64, F32), "rcv": sb(64, F32), "rt": sb(128, F32), "yl": sb(128, F32), "yi": sb(128, F32),
+    "res": sb(64, F32), "rt": sb(128, F32), "yl": sb(128, F32), "yi": sb(128, F32),
 }
 for _i in range(8):
     SCRATCH["ps%d" % _i] = ("psum", [128, 512], F32)
-SEMAPHORES = (["cv", "ca", "ct", "cg", "sl", "st", "sr"]
-              + ["%s%d" % (x, i) for x in ("sk", "rl", "rt", "rk", "rr") for i in range(NR)] + ["d%d" % i for i in range(48)])
-
-
-def shares(topo, src, dsts):
-    far = [d for d in dsts if not topo.mates(topo.chip(src), topo.chip(d))
-           and not topo.same_plane(topo.chip(src), topo.chip(d))]
-    order = far + [d for d in dsts if d not in far]
-    out = {}
-    at = 0
-    for i, d in enumerate(order):
-        e = topo.engines(src, d)
-        n = len(e) // 2 if i == 0 else len(e) // 4
-        out[d] = e[at:at + n]
-        at += n
-    return out
+SEMAPHORES = (["cv", "ca", "ct", "cg", "sent", "rw", "rn", "rg", "rq"] + ["rh%d" % i for i in range(NR)]
+              + ["d%d" % i for i in range(48)])
 
 
 def bits(engines):
     return sum(1 << e for e in engines)
 
 
+def far_first(topo, cores, me):
+    chip = topo.chip(cores[me])
+    others = [q for q in range(NR) if q != me]
+    mate = [q for q in others if topo.mates(chip, topo.chip(cores[q]))]
+    plane = [q for q in others if topo.same_plane(chip, topo.chip(cores[q]))]
+    return [q for q in others if q not in mate + plane] + plane + mate
+
+
+def helpers(topo, cores, me):
+    core = cores[me]
+    able = [c for c in topo.cores_of(core) if c != core and all(topo.may_write(c, d) for d in cores if d != core)]
+    return sorted(able, key=lambda c: topo.die(c) == topo.die(core))
+
+
+def dst(topo, d):
+    rid, pid, _ = topo.addr(d)
+    return DstId(rid=rid, pnc=pid)
+
+
+def quarter(T, me, k):
+    return T.win[:, M * me + 192 * k:M * me + 192 * k + 192]
+
+
+def spare(topo, cores, me):
+    off = topo.engines(cores[me], cores[(me + 1) % NR])
+    return [e for e in topo.engines(cores[me], helpers(topo, cores, me)[0]) if e not in off]
+
+
+def hand_on(g, core, T, topo):
+    cores = list(T.cores)
+    for me in range(NR):
+        hs = helpers(topo, cores, me)
+        if core in hs:
+            k = hs.index(core)
+            n = len(spare(topo, cores, me))
+            order = far_first(topo, cores, me)
+            eng = topo.engines(core, cores[order[0]])
+            w = quarter(T, me, k)
+            g.wait_ge(T.sem["rq"], n // 2 if k < 2 else n)
+            g.remote_dma_fused([RemoteDMATransfer(dst_ids=[dst(topo, cores[q]) for q in order], dma_engine_mask=bits(eng),
+                                                  remote_sem=T.sem["rw"], srcs=[w], dsts=[w for q in order])],
+                               local_sem=T.sem["sent"])
+            g.wait_ge(T.sem["sent"], len(eng))
+
+
 def rank_program(g, core, T, topo):
     me = T.rank_of(core)
     if me is None:
+        hand_on(g, core, T, topo)
         return
     cores = list(T.cores)
     others = [q for q in range(NR) if q != me]
-    mate = [q for q in others if topo.mates(topo.chip(core), topo.chip(cores[q]))]
-    plane = [q for q in others if topo.same_plane(topo.chip(core), topo.chip(cores[q]))]
-    order = [q for q in others if q not in mate + plane] + plane + mate
-    f, n, m = order
+    order = far_first(topo, cores, me)
+    hs = helpers(topo, cores, me)
+    near = spare(topo, cores, me)
+    nxt = (me + 1) % NR
+    eng = topo.engines(core, cores[order[0]])
+    half = len(eng) // 2
     q_of = {"g": g, "v": g.vector, "a": g.scalar, "t": g.tensor, "s": g.sync}
     csem = {"g": "cg", "v": "cv", "a": "ca", "t": "ct"}
     total = {}
@@ -100,7 +131,7 @@ def rank_program(g, core, T, topo):
         own = csem.get(q)
         evs = []
         for k in R:
-            evs += lastw.get(k, [])
+            evs += lastw[k]
         for k in W:
             evs += [e for e in lastw.get(k, []) + reads.get(k, []) if e[0] != own]
         wait(q, evs)
@@ -139,112 +170,142 @@ def rank_program(g, core, T, topo):
         for k in keys:
             lastw[k] = [(s, total[s])]
 
-    def dst(d):
-        rid, pid, _ = topo.addr(d)
-        return DstId(rid=rid, pnc=pid)
+    ranks = [cores[q] for q in order]
 
-    mine = shares(topo, core, [cores[q] for q in others])
-
-    def send(rsem, lsem, way, src_of, out, R):
+    def send(pieces, R):
         deps("g", R, [])
-        tr = [RemoteDMATransfer(dst_ids=[dst(cores[q])], dma_engine_mask=bits(e), remote_sem=T.sem["%s%d" % (rsem, me)],
-                                src=src_of(q), dst=out) for q, e in way]
-        g.remote_dma_fused(tr, local_sem=T.sem[lsem])
-        total[lsem] = total.get(lsem, 0) + sum(len(e) for q, e in way)
-
-    def got(q):
-        return len(shares(topo, cores[q], [c for c in cores if c != cores[q]])[core])
+        tr = [RemoteDMATransfer(dst_ids=[dst(topo, c) for c in to], dma_engine_mask=bits(e), remote_sem=T.sem[s],
+                                srcs=[i], dsts=[o for c in to]) for to, s, e, i, o in pieces]
+        g.remote_dma_fused(tr, local_sem=T.sem["sent"])
+        total["sent"] = total.get("sent", 0) + sum(len(x[2]) for x in pieces)
 
     v = g.vector
     pe = g.tensor
     ps = [T["ps%d" % i] for i in range(8)]
+    lf = T.hb[:, 144:208]
 
-    def load(q):
-        p = slice(32 * q, 32 * q + 32)
-        dma("s", T.kx[p, 0:6, :], T.kid[2 * q, :], [], ["kx0_%d" % q])
-        dma("a", T.kx[p, 6:12, :], T.kid[2 * q + 1, :], [], ["kx1_%d" % q])
+    def lcols(a, b):
+        return T.hb[:, 144 + a:144 + b]
 
+    dma("s", T.ht[:], T.tid[:], [], ["ht"])
     dma("a", T.lx[:], T.lett[:], [], ["lx"])
-    load(f)
-    dma("s", T.tbuf[:], T.tid[:], [], ["tbuf"])
-    for q in (n, m, me):
-        load(q)
-    dma("s", T.tin[me], T.tid[2 * me:2 * me + 2, :], [], ["tin%d" % me])
+    for h in range(2):
+        for x in range(8):
+            dma("sa"[x % 2], T.kx[:, h, x, :], T.kid[x, 16 * H * h:16 * H * (h + 1)], [], ["kx%d_%d" % (h, x)])
+    dma("s", T.n1x[:], T.kid[:, 16:32], [], ["n1x"])
 
     def iota(key, out, pattern, base, mult):
         comp("g", [], [key], lambda: g.iota(out, pattern, base, mult, allow_small_or_imprecise_dtypes=True))
 
-    comp("g", [], ["pi"], lambda: g.iota(T.pi[:], [[1, 1]], 0, 1))
-    iota("imk", T.imk[:], [[1, 143]], 0, -1)
-    iota("frk", T.frk[:], [[0, 4], [64, 2], [1, 16]], 0, -1)
-    comp("g", [], ["expi"], lambda: g.iota(T.expi[:], [[20, 4], [1, 4]], 0, 0))
-    send("rt", "st", [(q, mine[cores[q]]) for q in others], lambda q: T.tbuf[q], T.tin[me], ["tbuf"])
-
-    V([], ["tz0"], lambda: v.memset(T.tw[:, 0:512], 0.0))
-    act(["tz0"], ["tz1"], T.tw[:, 512:1024], T.tw[:, 0:512])
-    V(["pi"], ["pci"], lambda: v.tensor_scalar(T.pci[:], T.pi[:], 15, None, A.bitwise_and))
-    V(["pi"], ["sa"], lambda: v.tensor_scalar(T.sa[:], T.pi[:], 32.0, 128.0, A.is_lt, A.mult))
-    V(["pci"], ["pcf"], lambda: v.tensor_copy(T.pcf[:], T.pci[:]))
-    V(["imk"], ["ih"], lambda: v.tensor_scalar(T.ih[:], T.imk[:, 0:128], 0.0, None, A.is_equal))
-    V(["pcf"], ["zz"], lambda: v.tensor_scalar(T.zz[:], T.pcf[:], 0.0, None, A.is_equal))
-    V(["pcf"], ["k16"], lambda: v.tensor_scalar(T.k16[:], T.pcf[:], -1.0, 15.0, A.mult, A.add))
-    V(["sa", "zz"], ["sk"], lambda: v.tensor_scalar(T.sk[:], T.sa[:], -16.0, T.zz[:], A.add, A.mult))
-    act(["lx"], ["lf"], T.lf[:], T.lx[:])
-    dma("s", T.lbuf[:], T.lf[:], ["lf"], ["lbuf"])
-    dma("s", T.lin[me], T.lf[32 * me:32 * me + 32, :], ["lf"], ["lin%d" % me])
-    tz = ["tz%d" % x for x in range(6)]
-
-    code = float(M * me) - OFF
-    eng = topo.engines(core, cores[f])
-
-    def cast(q):
-        p = slice(32 * q, 32 * q + 32)
-        V(["kx0_%d" % q], ["kh0_%d" % q], lambda: v.tensor_copy(T.kh[p, :, 0:64], T.kx[p, 0:6, :]))
-        act(["kx1_%d" % q], ["kh1_%d" % q], T.kh[p, :, 64:128], T.kx[p, 6:12, :])
-
-    def turn(q):
-        p = slice(32 * q, 32 * q + 32)
-        comp("t", ["kh0_%d" % q, "kh1_%d" % q, "ih"], ["ps%d" % q],
-             [lambda b=b: pe.matmul(ps[q][:, b:192:6], T.kh[p, b, :], T.ih[p, p], True, True) for b in range(6)])
-
-    def leave(q, by):
-        o, i = T.ks[:, 192 * q:192 * q + 192], ps[q][:, 0:192]
-        if by == "v":
-            V(["ps%d" % q], ["ks%d" % q], lambda: v.tensor_scalar(o, i, code, None, A.add))
+    def equal(key, out, cols, x, y=None, R=()):
+        if y is None:
+            V(["imk"] + list(R), [key], lambda: v.tensor_scalar(out, T.imk[:, 0:cols], x, None, A.is_equal))
         else:
-            comp("a", ["ps%d" % q], ["ks%d" % q], lambda: g.scalar.activation(o, i, F.Copy, bias=code))
+            V(["imk"] + list(R), [key], lambda: v.tensor_scalar(out, T.imk[:, 0:cols], x, y, A.is_equal, A.mult))
 
-    def go(q):
-        send("rk", "sk%d" % q, [(q, eng)], lambda d: T.ks[:, 192 * d:192 * d + 192], T.kin[:, 192 * me:192 * me + 192],
-             ["ks%d" % q])
+    def zero(q):
+        V([], ["tz%d" % q], lambda: v.memset(T.tw[:, M * q:M * q + M], 0.0))
 
-    cast(f)
-    turn(f)
-    cast(n)
-    leave(f, "v")
-    go(f)
-    send("rl", "sl", [(d, mine[cores[d]]) for d in others], lambda d: T.lbuf[d], T.lin[me], ["lbuf"])
-    turn(n)
-    cast(m)
-    turn(m)
-    leave(n, "a")
-    go(n)
-    cast(me)
-    turn(me)
-    leave(m, "v")
-    go(m)
-    leave(me, "a")
-    act(["tz0"], ["tz3"], T.tw[:, 1536:2048], T.tw[:, 0:512])
-    for q in others:
-        arrive("rl%d" % q, got(q), ["lin%d" % q])
-        arrive("rt%d" % q, got(q), ["tin%d" % q])
-        arrive("rk%d" % q, len(eng), ["kin%d" % q])
-
-    iota("e8i", T.e8i[0:8, :], [[1, 8], [0, 16]], 0, -1)
-    iota("tz5", T.tw[:, 2304:3072], [[0, 768]], 0, 0)
+    iota("imk", T.imk[:], [[1, 143]], 0, -1)
+    comp("g", [], ["pi"], lambda: g.iota(T.pi[:], [[1, 1]], 0, 1))
+    comp("g", [], ["expi"], lambda: g.iota(T.expi[:], [[1, 4]], 4 * me, 0))
     iota("one", T.one[:], [[0, 128]], 1, 0)
-    comp("g", ["one"], ["ib"], lambda: g.affine_select(T.ib[:], T.one[:], [[1, 128]], A.is_equal, 0.0, 0, -1))
-    comp("g", ["one"], ["shb"], lambda: g.affine_select(T.shb[:], T.one[:], [[1, 128]], A.is_equal, 0.0, -3, -1))
+
+    zero(me)
+    act(["tz%d" % me], ["tz%d" % order[0]], T.tw[:, M * order[0]:M * order[0] + M], T.tw[:, M * me:M * me + M])
+    equal("ih", T.ih[:], 128, 0.0)
+    equal("ihn", T.ihn[:], 128, 0.0, -1.0)
+    equal("shb", T.shb[:], 128, 3.0)
+    V(["pi"], ["pci"], lambda: v.tensor_scalar(T.pci[:], T.pi[:], 15, None, A.bitwise_and))
+    V(["expi"], ["expu"], lambda: v.tensor_copy(T.expu[:], T.expi[:]))
+    V(["pci"], ["pcf"], lambda: v.tensor_copy(T.pcf[:], T.pci[:]))
+    zero(order[2])
+
+    act(["ht"], ["hb0"], T.hb[:, 0:48], T.ht[:])
+    comp("a", ["ht"], ["hb2"], lambda: g.scalar.activation(T.hb[:, 96:144], T.ht[:], F.Sign))
+    act(["lx"], ["lf"], lf, T.lx[:])
+    V(["ht", "hb0"], ["hb1"], lambda: v.tensor_tensor(T.hb[:, 48:96], T.ht[:], T.hb[:, 0:48], A.subtract))
+    send([(ranks, "rh%d" % me, eng, T.hb[:, 0:160], T.hin[:, me, :])], ["hb0", "hb1", "hb2", "lf"])
+    for q in others:
+        arrive("rh%d" % q, len(eng), ["hin%d" % q])
+    tws = {q: ["tw%d_%d" % (q, x) for x in range(3)] for q in range(NR)}
+
+    def planes(q):
+        for x in (0, 2, 1):
+            deps("s", ["tz%d" % q], [])
+            i, R = (T.hb[:, 48 * x:48 * x + 48], ["hb%d" % x]) if q == me else (T.hin[:, q, 48 * x:48 * x + 48], ["hin%d" % q])
+            dma("s", T.tw[x:128:16, M * q:M * q + M], i, R, [tws[q][x]])
+
+    planes(me)
+    dma("s", T.lu[0:8, 0:1024], lf, ["lf"], ["lua"])
+    comp("g", ["one"], ["e8"], lambda: g.affine_select(T.e8[0:8, :], T.one[0:8, :], [[1, 8], [0, 16]], A.is_equal, 0.0, 0, -1))
+    comp("g", ["one"], ["sel"], lambda: g.affine_select(T.sel[:], T.one[:], [[16, 8], [0, 16]], A.is_equal, 0.0, 0, -1))
+
+    def cast(h):
+        R = ["kx%d_%d" % (h, x) for x in range(8)]
+        for j in range(3):
+            i = T.kx[:, h, :, 16 * j:16 * j + 16]
+            V(R, ["kc%d%d" % (h, j)], lambda: v.tensor_scalar(T.kc[:, h, j, :], i, LO, HI, A.max, A.min))
+            comp("a", R, ["kh%d%d" % (h, j)],
+                 lambda: g.scalar.activation(T.kh[:, h, j, :], i, F.Copy, bias=-float(H), scale=2.0))
+
+    def turn(h):
+        for j in range(3):
+            for s in range(2):
+                o = ps[2 * h + s][:, j:192:3]
+                comp("t", ["kc%d%d" % (h, j), "kh%d%d" % (h, j), "ih", "ihn"], ["ps%d" % (2 * h + s)],
+                     [lambda: pe.matmul(o, T.kh[:, h, j, :], T.ih[:, 64 * s:64 * s + 64], True, False),
+                      lambda: pe.matmul(o, T.kc[:, h, j, :], T.ihn[:, 64 * s:64 * s + 64], False, True)])
+
+    def leave(h):
+        a = M * me + H * h
+        V(["ps%d" % (2 * h)], ["w%da" % h], lambda: v.tensor_copy(T.win[:, a:a + 192], ps[2 * h][:, 0:192]))
+        act(["ps%d" % (2 * h + 1)], ["w%db" % h], T.win[:, a + 192:a + H], ps[2 * h + 1][:, 0:192])
+
+    own = ["w0a", "w0b", "w1a", "w1b"]
+
+    def go(ks):
+        n = len(near) // len(ks)
+        send([([hs[k]], "rq", near[n * x:n * x + n], quarter(T, me, k), quarter(T, me, k)) for x, k in enumerate(ks)],
+             [own[k] for k in ks])
+
+    blk = T.win[:, M * me:M * me + M]
+    tblk = T.tw[:, M * me:M * me + M]
+
+    cast(0)
+    turn(0)
+    V(["n1x"], ["n1u"], lambda: v.tensor_copy(T.n1u[:, 0:1], T.n1x[:]))
+    cast(1)
+    turn(1)
+    leave(0)
+    go([0, 1])
+    zero(order[1])
+    act(tws[me] + ["n1u"], ["g1"], T.g1[:], tblk.indirect(T.n1u[:, 0:1]))
+    act(["g1", "expu"], ["g1e"], T.g1e[:], T.g1[:].indirect(T.expu[:]))
+    comp("t", ["g1e", "shb"], ["ps4"], lambda: pe.matmul(ps[4][:, 0:64], T.shb[:], T.g1e[:], True, True))
+    leave(1)
+    go([2])
+    act(["ps4"], ["g1s"], T.g1s[:], ps[4][:, 0:64])
+
+    w1 = blk.indirect(T.n1u[:, 0:1])
+    V(own + ["n1u"], ["c2"], lambda: v.tensor_scalar(T.c2[:], w1, 256.0, -256.0, A.min, A.max))
+    V(own + ["n1u", "c2"], ["s2"], lambda: v.tensor_tensor(T.s2[:], w1, T.c2[:], A.add))
+    V(["s2"], ["n2u"], lambda: v.tensor_scalar(T.n2u[:], T.s2[:], 0.5, float(H), A.mult, A.add))
+    n2 = T.n2u[:, 4 * me:4 * me + 4]
+    nw, g12 = T.nw[:, 64 * me:64 * me + 64], T.g12[:, 64 * me:64 * me + 64]
+    act(own + ["n2u"], ["nw"], nw, blk.indirect(n2))
+    V(tws[me] + ["n2u", "g1s"], ["g12"], lambda: v.tensor_tensor(g12, tblk.indirect(n2), T.g1s[:], A.add))
+    send([(ranks, "rn", eng, nw, nw)], ["nw"])
+    send([(ranks, "rg", eng, g12, g12)], ["g12"])
+    send([(ranks, "rw", eng, quarter(T, me, 3), quarter(T, me, 3))], [own[3]])
+    arrive("rw", 4 * len(eng) * len(others), ["win"])
+    arrive("rn", len(eng) * len(others), ["nwin"])
+    arrive("rg", len(eng) * len(others), ["g12in"])
+
+    for q in order[::-1]:
+        planes(q)
+    tall = [k for q in range(NR) for k in tws[q]]
+
     iota("vt", T.vt[:], [[0, 32]], 0, 0)
 
     def weight(j, k, x, w):
@@ -257,143 +318,45 @@ def rank_program(g, core, T, topo):
     weight(0, 1, 5, K17)
     for j in range(1, 4):
         weight(j, j + 1, 2, (j + 1) * K17)
-    iota("pdi", T.pdi[:], [[1, 2], [2, 64]], 0, -1)
-
-    lins = ["lin%d" % q for q in range(4)]
-    tins = ["tin%d" % q for q in range(4)]
-    for x in range(4):
-        dma("s", T.ht[16 * x:16 * x + 16, :], T.tin[:, 64 * (x % 2):64 * (x % 2) + 64, :], tins, ["ht%d" % x])
-    dma("s", T.lu[0:8, 0:1024], T.lin[:], lins, ["lua"])
-    dma("s", T.lu[0:6, 1024:1040], T.lin[1:4, 0::64, :], lins, ["lub"])
-    dma("s", T.lu[6:8, 1024:1040], T.lin[0, 0::64, :], lins, ["luc"])
-    lus = ["lua", "lub", "luc"]
-
-    def sums(q, ka, kb, va):
-        src, keys = (T.ks, ["ks%d" % me]) if q == me else (T.kin, ["kin%d" % q])
-        c = 192 * q
-        for k, a, b in ((ka, 0, va // 4), (kb, va // 4, 192)):
-            comp("t", keys + ["r%d" % x for x in range(4)], ["ps%d" % k],
-                 [lambda x=x: pe.matmul(ps[k][:, x:4 * (b - a):4], T["r%d" % x][:], src[:, c + a:c + b], True, True)
-                  for x in range(4)])
-
-    def copyv(q, ka, va):
-        V(["ps%d" % ka], ["wa%d" % q], lambda: v.tensor_copy(T.win[:, M * q:M * q + va], ps[ka][:, 0:va]))
-
-    def copya(q, kb, va):
-        act(["ps%d" % kb], ["wb%d" % q], T.win[:, M * q + va:M * q + M], ps[kb][:, 0:M - va])
-
-    def block(q):
-        return T.win[:, M * q:M * q + M], T.tw[:, M * q:M * q + M], OFF - M * q
-
-    def table1(q):
-        V(["wa%d" % q], ["n1_%d" % q],
-          lambda: v.tensor_scalar(T.n1u[:, 2 * q:2 * q + 1], T.win[:, M * q + 1:M * q + 2], block(q)[2], None, A.add))
-
-    def table2(q, by="v"):
-        R, o, i = ["wa%d" % q, "wb%d" % q, "n1_%d" % q], T.n2u[:, 16 * q:16 * q + 16], T.n1u[:, 2 * q:2 * q + 1]
-        if by == "v":
-            V(R, ["n2_%d" % q], lambda: v.tensor_scalar(o, block(q)[0].indirect(i), block(q)[2], None, A.add))
-        else:
-            comp("a", R, ["n2_%d" % q], lambda: g.scalar.activation(o, block(q)[0].indirect(i), F.Copy, bias=block(q)[2]))
-
-    def table3(q, by="v"):
-        R, o, i = ["wa%d" % q, "wb%d" % q, "n2_%d" % q], T.nw[:, 64 * q:64 * q + 64], T.n2u[:, 20 * q:20 * q + 4]
-        if by == "v":
-            V(R, ["nw%d" % q], lambda: v.tensor_copy(o, block(q)[0].indirect(i)))
-        else:
-            act(R, ["nw%d" % q], o, block(q)[0].indirect(i))
-
-    tws = []
-
-    def idlists(q):
-        act(tws + ["n1_%d" % q], ["g1_%d" % q], T.g1[:, 16 * q:16 * q + 16], block(q)[1].indirect(T.n1u[:, 2 * q:2 * q + 1]))
-        act(tws + ["n2_%d" % q], ["g2_%d" % q], T.g2[:, 64 * q:64 * q + 64],
-            block(q)[1].indirect(T.n2u[:, 20 * q:20 * q + 4]))
-
-    for x in range(4):
-        V(["frk"], ["r%d" % x], lambda: v.tensor_scalar(T["r%d" % x][:], T.frk[:], float(-16 * x), None, A.is_equal))
-    sums(me, 4, 5, SA)
-    V(["expi"], ["expu"], lambda: v.tensor_copy(T.expu[:], T.expi[:]))
-    V(["imk"], ["llz"], lambda: v.tensor_scalar(T.ll[:], T.imk[:, 0:136], 0.0, None, A.mult))
-    V([], ["tz2"], lambda: v.memset(T.tw[:, 1024:1536], 0.0))
-    copyv(me, 4, SA)
-    copya(me, 5, SA)
-    comp("a", ["ih"], ["i16"], lambda: g.scalar.activation(T.i16[:], T.ih[:], F.Copy, scale=16.0))
-    V(["imk", "sk"], ["sh1"], lambda: v.tensor_scalar(T.sh1[:], T.imk[:, 0:128], 1.0, T.sk[:], A.add, A.is_equal))
-    V(["imk", "k16"], ["t1h"], lambda: v.tensor_scalar(T.t1h[:], T.imk[:], T.k16[:], None, A.is_equal))
-    deps("s", ["llz"], [])
-    dma("s", T.ll[:, 64:128], T.lin[:], lins, ["ll"])
-    table1(me)
-    table2(me)
-    table3(me)
-    V([], ["tz4"], lambda: v.memset(T.tw[:, 2048:2304], 0.0))
-    V(["e8i"], ["e8"], lambda: v.tensor_scalar(T.e8[0:8, :], T.e8i[0:8, :], 0.0, None, A.is_equal))
-
-    sums(f, 6, 7, SF)
-    copyv(f, 6, SF)
-    copya(f, 7, SF)
-    table1(f)
-
-    hts = ["ht%d" % x for x in range(4)]
-    act(hts, ["hb0"], T.hb[0:64, 0:192], T.ht[0:64, :])
-    comp("a", hts, ["hb2"], lambda: g.scalar.activation(T.hb[0:64, 384:576], T.ht[0:64, :], F.Sign))
-    V(hts + ["hb0"], ["hb1"], lambda: v.tensor_tensor(T.hb[0:64, 192:384], T.ht[0:64, :], T.hb[0:64, 0:192], A.subtract))
-    for x in (0, 2, 1):
-        for s in range(2):
-            deps("s", tz, [])
-            dma("s", T.tw[64 * s + x:64 * s + 64:16, :], T.hb[0:64, 192 * x:192 * x + 192], ["hb%d" % x],
-                ["tw%d%d" % (x, s)])
-            tws.append("tw%d%d" % (x, s))
+    iota("onf", T.onf[:], [[0, 128]], 1, 0)
+    comp("g", ["onf"], ["id"], lambda: g.affine_select(T["id"][:], T.onf[:], [[1, 2], [2, 64]], A.is_equal, 0.0, 0, -1))
 
     def letters(k):
-        comp("t", ["lua", "e8"], ["ps%d" % (2 + k)],
-             [lambda s=s: pe.matmul(ps[2 + k][:, s:512:8], T.e8[0:8, :], T.lu[0:8, 128 * s + 64 * k:128 * s + 64 * k + 64],
+        comp("t", ["lua", "e8"], ["ps%d" % (6 + k)],
+             [lambda s=s: pe.matmul(ps[6 + k][:, s:512:8], T.e8[0:8, :], T.lu[0:8, 128 * s + 64 * k:128 * s + 64 * k + 64],
                                     True, True) for s in range(8)])
 
     def mask(k):
-        V(["ps%d" % (2 + k), "pcf"], ["em%d" % k],
-          lambda: v.tensor_scalar(T.em[:, k:1024:2], ps[2 + k][:, 0:512], T.pcf[:], None, A.is_equal))
+        V(["ps%d" % (6 + k), "pcf"], ["em%d" % k],
+          lambda: v.tensor_scalar(T.em[:, k:1024:2], ps[6 + k][:, 0:512], T.pcf[:], None, A.is_equal))
 
-    def more():
-        comp("t", lus + ["e8"], ["ps0"],
-             [lambda e=e: pe.matmul(ps[0][:, 16 * e:16 * e + 16], T.e8[0:8, :], T.lu[0:8, 64 + e:64 + e + 961:64], True, True)
-              for e in range(3)])
-        comp("t", ["ll", "llz", "i16", "ih", "sh1"], ["ps1"],
-             [lambda: pe.matmul(ps[1][:, 0:64], T.i16[:], T.ll[:, 64:128], True, False),
-              lambda: pe.matmul(ps[1][:, 0:64], T.ih[:], T.ll[:, 65:129], False, False),
-              lambda: pe.matmul(ps[1][:, 0:64], T.sh1[:], T.ll[:, 1:65], False, True)])
-
-    ems = ["em0", "em1", "em2"]
-
-    sums(n, 4, 5, SN)
-    copyv(n, 4, SN)
-    copya(n, 5, SN)
     letters(0)
     letters(1)
-    more()
-    sums(m, 6, 7, SM)
-    table1(n)
+    equal("ib", T.ib[:], 128, 0.0)
+    V(["pcf"], ["zz"], lambda: v.tensor_scalar(T.zz[:], T.pcf[:], 0.0, None, A.is_equal))
+    V(["pcf"], ["nz"], lambda: v.tensor_scalar(T.nz[:], T.pcf[:], 0.0, None, A.not_equal))
+    V(["pcf"], ["k16"], lambda: v.tensor_scalar(T.k16[:], T.pcf[:], -1.0, 15.0, A.mult, A.add))
+    comp("a", ["ib"], ["i16"], lambda: g.scalar.activation(T.i16[:], T.ib[:], F.Copy, scale=16.0))
+    equal("sh", T.sh[:], 128, -1.0, T.nz[:], ["nz"])
+    equal("sh15", T.sh15[:], 128, 15.0, T.zz[:], ["zz"])
     mask(0)
-    table2(f, "a")
-    table3(f, "a")
     mask(1)
-    act(["ps1"], ["cu"], T.cu[:], ps[1][:, 0:64])
-    V(["ps0", "pcf"], ["em2"], lambda: v.tensor_scalar(T.em[:, 1024:1072], ps[0][:, 0:48], T.pcf[:], None, A.is_equal))
-    copyv(m, 6, SM)
-    copya(m, 7, SM)
-    table2(n)
-    table1(m)
-    table3(n)
-    table2(m)
-    table3(m)
-    for q in (me, f, n, m):
-        idlists(q)
-    act(["g1_%d" % q for q in range(4)] + ["expu"], ["g1e"], T.g1e[:], T.g1[:, 0:64].indirect(T.expu[:, 0:16]))
-    wk = ["w%s%d" % (x, q) for q in range(4) for x in "ab"]
-    nws = ["nw%d" % q for q in range(4)]
-    g2s = ["g2_%d" % q for q in range(4)]
-    win = T.win[:, 0:3072]
-    twin = T.tw[:, 0:3072]
+    comp("t", ["lf", "hin%d" % nxt, "i16", "ib", "sh", "sh15"], ["ps5"],
+         [lambda: pe.matmul(ps[5][:, 0:63], T.i16[:], lcols(0, 63), True, False),
+          lambda: pe.matmul(ps[5][:, 0:63], T.ib[:], lcols(1, 64), False, True),
+          lambda: pe.matmul(ps[5][:, 63:64], T.i16[:], lcols(63, 64), True, False),
+          lambda: pe.matmul(ps[5][:, 63:64], T.sh[:], lcols(0, 1), False, False),
+          lambda: pe.matmul(ps[5][:, 63:64], T.sh15[:], T.hin[:, nxt, 144:145], False, True)])
+    comp("t", ["lua", "e8", "sel", "hin%d" % nxt], ["ps4"],
+         [lambda e=e: pe.matmul(ps[4][:, 16 * e:16 * e + 15], T.e8[0:8, :], T.lu[0:8, 64 + e:1024:64], True, True)
+          for e in range(3)]
+         + [lambda: pe.matmul(ps[4][:, 15:48:16], T.sel[:], T.hin[:, nxt, 144:147], True, True)])
+    act(["ps5"], ["cu"], T.cu[:], ps[5][:, 0:64])
+    V(["ps4", "pcf"], ["em2"], lambda: v.tensor_scalar(T.em[:, 1024:1072], ps[4][:, 0:48], T.pcf[:], None, A.is_equal))
+    equal("t1h", T.t1h[:], 143, T.k16[:], 0.5, ["k16"])
+    V(["lx"], ["ow"], lambda: v.tensor_scalar(T.ow[:], T.lx[:], 2, None, A.arith_shift_right))
+    V(["ow"], ["off"], lambda: v.tensor_scalar(T.off[:], T.ow[:], float(M), float(H), A.mult, A.add))
+    ems = ["em0", "em1", "em2"]
 
     portions = ((0, CUT), (CUT, 1024))
 
@@ -409,9 +372,13 @@ def rank_program(g, core, T, topo):
                                     i == 15) for i in range(16)])
 
     def lists(bank, nm, h):
-        a, b = portions[h]
-        V(["ps%d" % bank], ["%s%d" % (nm, h)],
-          lambda: v.tensor_scalar(T[nm][:, a // 16:b // 16], ps[bank][:, 0:(b - a) // 16], OFF, None, A.add))
+        a, b = portions[h][0] // 16, portions[h][1] // 16
+        o = 64 * (nm == "n4u")
+        key = "%s%d" % (nm, h)
+        c, s, p = T.lc[:, o + a:o + b], T.ls[:, o + a:o + b], ps[bank][:, 0:b - a]
+        V(["ps%d" % bank], ["c" + key], lambda: v.tensor_scalar(c, p, 128.0, -128.0, A.min, A.max))
+        V(["ps%d" % bank, "off"], ["s" + key], lambda: v.tensor_tensor(s, p, T.off[:, a:b], A.add))
+        V(["c" + key, "s" + key], [key], lambda: v.tensor_tensor(T[nm][:, a:b], s, c, A.add))
 
     pieces = {"i12": [], "i3": [], "i4": []}
 
@@ -429,47 +396,33 @@ def rank_program(g, core, T, topo):
              [lambda s=s: pe.matmul(ps[bank][:, s:64 * x:8], T[rep][:, s:1024:8], T.vt[:, 8 * j:8 * j + 8 * x], True, True)
               for s in range(8)])
 
-    walk("p3", 0, T.nw[:, 0:256], T.cu, 2, nws + ["cu"])
-    comp("t", ["g1e", "shb", "ib"] + g2s, ["ps0"],
-         [lambda: pe.matmul(ps[0][:, 0:256], T.shb[:], T.g1e[:], True, False),
-          lambda: pe.matmul(ps[0][:, 0:256], T.ib[:], T.g2[:], False, True)])
-    act(["ps0"], ["g12"], T.g12[:], ps[0][:, 0:256])
-    nodes(4, "p3", 0)
-    walk("p3", 1, T.nw[:, 0:256], T.cu, 2, nws + ["cu"])
-    nodes(5, "p3", 1)
-    for a in (0, 512):
-        ids("a", "i12", T.g12[:, 0:256], T.cu, a, a + 512, ["g12", "cu"])
+    win, twin = T.win[:, 0:3072], T.tw[:, 0:3072]
     for h in range(2):
-        lists(4 + h, "n3u", h)
-        walk("p4", h, win, T.n3u, 3, wk + ["n3u%d" % h])
-        nodes(6 + h, "p4", h)
-        ids("a", "i3", twin, T.n3u, portions[h][0], portions[h][1], tws + ["n3u%d" % h])
-    value("i12", 1, 2, 0)
-    value("i3", 3, 1, 2)
-    lists(6, "n4u", 0)
-    ids("v", "i4", twin, T.n4u, 0, CUT, tws + ["n4u0"])
-    lists(7, "n4u", 1)
-    ids("v", "i4", twin, T.n4u, CUT, IV, tws + ["n4u1"])
-    ids("a", "i4", twin, T.n4u, IV, 1024, tws + ["n4u1"])
-    V(["ps1"], ["b1"], lambda: v.tensor_copy(T.b1[:], ps[1][:, 64:128]))
-    V(["ps1", "b1"], ["b2"], lambda: v.tensor_tensor(T.b2[:], ps[1][:, 0:64], T.b1[:], A.max))
-    value("i4", 0, 1, 3)
-    V(["ps3", "b2"], ["b3"], lambda: v.tensor_tensor(T.b3[:], ps[3][:, 0:64], T.b2[:], A.max))
-    V(["ps0", "b3"], ["res"], lambda: v.tensor_tensor(T.res[:], ps[0][:, 0:64], T.b3[:], A.max))
-    V(["res"], ["rcv%d" % me],
-      lambda: v.tensor_copy(T.rcv[:, 16 * me:16 * me + 16], T.res[:, 16 * me:16 * me + 16]))
-    V(["pdi"], ["id"], lambda: v.tensor_scalar(T["id"][:], T.pdi[:], 0.0, None, A.is_equal))
+        walk("p3", h, T.nw[:, 0:256], T.cu, 2, ["nw", "nwin", "cu"])
+        nodes(h, "p3", h)
+    ids("a", "i12", T.g12[:, 0:256], T.cu, 0, 1024, ["g12", "g12in", "cu"])
+    for h in range(2):
+        lists(h, "n3u", h)
+        walk("p4", h, win, T.n3u, 3, own + ["win", "n3u%d" % h])
+        nodes(2 + h, "p4", h)
+        ids("a", "i3", twin, T.n3u, portions[h][0], portions[h][1], tall + ["n3u%d" % h])
+    value("i12", 4, 2, 0)
+    value("i3", 5, 1, 2)
+    lists(2, "n4u", 0)
+    ids("v", "i4", twin, T.n4u, 0, CUT, tall + ["n4u0"])
+    lists(3, "n4u", 1)
+    ids("v", "i4", twin, T.n4u, CUT, IV, tall + ["n4u1"])
+    ids("a", "i4", twin, T.n4u, IV, 1024, tall + ["n4u1"])
+    V(["ps4"], ["b1"], lambda: v.tensor_copy(T.b1[:], ps[4][:, 64:128]))
+    V(["ps4", "b1"], ["b2"], lambda: v.tensor_tensor(T.b2[:], ps[4][:, 0:64], T.b1[:], A.max))
+    value("i4", 6, 1, 3)
+    V(["ps5", "b2"], ["b3"], lambda: v.tensor_tensor(T.b3[:], ps[5][:, 0:64], T.b2[:], A.max))
+    V(["ps6", "b3"], ["res"], lambda: v.tensor_tensor(T.res[:], ps[6][:, 0:64], T.b3[:], A.max))
 
-    half = len(eng) // 2
-    for way in ([(f, eng)], [(n, eng[:half]), (m, eng[half:])]):
-        send("rr", "sr", way, lambda d: T.res[:, 16 * d:16 * d + 16], T.rcv[:, 16 * me:16 * me + 16], ["res"])
-    for q in others:
-        arrive("rr%d" % q, len(eng) if q == f else half, ["rcv%d" % q])
-    p = ps[5][0:64, 0:128]
-    comp("t", ["rcv%d" % q for q in range(4)] + ["id"], ["ps5"],
-         lambda: pe.matmul(p, T.rcv[:], T["id"][:], True, True))
-    V(["ps5"], ["rt"], lambda: v.tensor_scalar(T.rt[0:64, :], p, RND, RND, A.add, A.subtract))
-    V(["ps5", "rt"], ["yi"], lambda: v.tensor_tensor(T.yi[0:64, :], p, T.rt[0:64, :], A.subtract))
+    p = ps[7][0:64, 0:128]
+    comp("t", ["res", "id"], ["ps7"], lambda: pe.matmul(p, T.res[:], T["id"][:], True, True))
+    V(["ps7"], ["rt"], lambda: v.tensor_scalar(T.rt[0:64, :], p, RND, RND, A.add, A.subtract))
+    V(["ps7", "rt"], ["yi"], lambda: v.tensor_tensor(T.yi[0:64, :], p, T.rt[0:64, :], A.subtract))
     comp("a", ["rt"], ["yl"], lambda: g.scalar.activation(T.yl[0:64, :], T.rt[0:64, :], F.Copy, scale=1.0 / K17))
     for hi in range(2):
         dma("s", T.yid[:, 512 * hi:512 * hi + 512], T.yi[0:64, 64 * hi:64 * hi + 64], ["yi"], ["oi%d" % hi])

@@ -6,8 +6,24 @@ NR = 4
 M = 768
 H = 384
 LO, HI = 128.0, 640.0
-CUT = 512
-IV = 800
+CL = 128.0
+P4 = 1024
+AT = [0, 3, 6]
+QS = ["asasasas"] * 3
+IO = (0, 1, 2)
+LFQ = "v"
+L3 = "aa"
+BP = (1, 2, 2)
+VP = 1
+I12 = 1024
+LATE = False
+ZA = 256
+LF = 0
+SELF = -1
+IDS = [0, 1, 2]
+PLAN = [[(SELF, 0, 160), (0, 160, 320)], [(1, 320, 480), (2, 480, 640)], [(SELF, 640, 768)]]
+MERGE = False
+IV = 928
 K17 = 131072.0
 RND = 12582912.0 * K17
 HF = "float16"
@@ -22,27 +38,29 @@ def sb(cols, dtype):
 
 
 SCRATCH = {
-    "lx": sb(64, I32), "ht": sb(48, I32), "n1x": sb(1, I32), "hb": sb(208, BF), "hin": sb([4, 160], BF),
-    "kx": sb([2, 8, 48], I32), "kh": sb([2, 3, 128], HF), "kc": sb([2, 3, 128], HF),
+    "lx": sb(64, I32), "ht": sb(48, I32), "n1x": sb(1, I32), "hb": sb(208, BF), "hin": sb([4, 144], BF),
+    "hx": sb(8, BF), "le": sb(8, BF), "ab": sb(512, BF), "ab2": sb(48, BF), "ncf": sb(1, F32),
+    "kx": sb([8, 96], I32), "kh": sb([6, 128], HF), "kc": sb([6, 128], HF),
     "win": sb(3072, BF), "tw": sb(3072, BF), "nw": sb(256, BF), "g12": sb(256, BF),
-    "lu": sb(1024, BF), "sel": sb(128, BF), "em": sb(1072, BF),
-    "pi": sb(1, I32), "pci": sb(1, I32), "pcf": sb(1, F32), "k16": sb(1, F32), "zz": sb(1, F32), "nz": sb(1, F32),
-    "imk": sb(143, BF), "one": sb(128, BF), "onf": sb(128, F32),
+    "lu": sb(1032, BF), "em": sb(1072, BF),
+    "pi": sb(1, I32), "pci": sb(1, I32), "pcf": sb(1, F32), "zz": sb(1, F32), "nz": sb(1, F32),
+    "imk": sb(128, BF), "one": sb(128, BF), "wb": sb(16, BF),
     "expi": sb(4, I32), "expu": sb(4, U16),
     "e8": sb(128, BF), "ih": sb(128, HF), "ihn": sb(128, HF), "ib": sb(128, BF), "i16": sb(128, BF),
-    "sh": sb(128, BF), "sh15": sb(128, BF), "shb": sb(128, BF), "t1h": sb(143, BF), "vt": sb(32, BF), "id": sb(128, F32),
-    "ow": sb(64, I32), "off": sb(64, F32),
+    "sh": sb(128, BF), "sh15": sb(128, BF), "shb": sb(128, BF), "vt": sb(32, BF), "id": sb(128, F32),
+    "ow": sb(64, I32), "off": sb(64, BF),
     "cu": sb(64, U16), "n1u": sb(2, U16), "n2u": sb(16, U16), "n3u": sb(64, U16), "n4u": sb(64, U16),
-    "c2": sb(16, F32), "s2": sb(16, F32), "lc": sb(128, F32), "ls": sb(128, F32),
+    "c2": sb(16, F32), "s2": sb(16, F32), "zb": sb([2, 128], BF), "zc": sb([2, 128], BF),
+    "g32": sb(32, BF), "r32": sb(32, BF), "ai": sb(128, BF), "dm": sb(128, BF), "p4i": sb(1, I32), "p4f": sb(1, F32),
     "p3": sb(1024, BF), "p4": sb(1024, BF),
     "g1": sb(16, BF), "g1e": sb(64, BF), "g1s": sb(64, BF),
     "i12": sb(1024, BF), "i3": sb(1024, BF), "i4": sb(1024, BF),
     "b1": sb(64, F32), "b2": sb(64, F32), "b3": sb(64, F32),
-    "res": sb(64, F32), "rt": sb(128, F32), "yl": sb(128, F32), "yi": sb(128, F32),
+    "res": sb(64, F32), "rt": sb(64, F32), "yl": sb(64, F32), "yi": sb(64, F32),
 }
 for _i in range(8):
     SCRATCH["ps%d" % _i] = ("psum", [128, 512], F32)
-SEMAPHORES = (["cv", "ca", "ct", "cg", "sent", "rw", "rn", "rg", "rq"] + ["rh%d" % i for i in range(NR)]
+SEMAPHORES = (["cv", "ca", "ct", "cg", "sent", "rw", "rn", "rg", "rq0", "rq1", "rq2", "rq3", "rp", "rx"] + ["rh%d" % i for i in range(NR)]
               + ["d%d" % i for i in range(48)])
 
 
@@ -69,13 +87,23 @@ def dst(topo, d):
     return DstId(rid=rid, pnc=pid)
 
 
-def quarter(T, me, k):
-    return T.win[:, M * me + 192 * k:M * me + 192 * k + 192]
-
-
 def spare(topo, cores, me):
     off = topo.engines(cores[me], cores[(me + 1) % NR])
     return [e for e in topo.engines(cores[me], helpers(topo, cores, me)[0]) if e not in off]
+
+
+def deal(call, near, eng):
+    k = len([c for c, a, b in call if c != SELF])
+    share = {0: [], 1: [1], 2: [2, 2], 3: [2, 4, 4], 4: [4, 4, 4, 4]}[k]
+    out, at = [], 0
+    for c, a, b in call:
+        if c == SELF:
+            out.append(eng)
+        else:
+            n = len(near) // share.pop(0)
+            out.append(near[at:at + n])
+            at += n
+    return out
 
 
 def hand_on(g, core, T, topo):
@@ -87,12 +115,19 @@ def hand_on(g, core, T, topo):
             n = len(spare(topo, cores, me))
             order = far_first(topo, cores, me)
             eng = topo.engines(core, cores[order[0]])
-            w = quarter(T, me, k)
-            g.wait_ge(T.sem["rq"], n // 2 if k < 2 else n)
-            g.remote_dma_fused([RemoteDMATransfer(dst_ids=[dst(topo, cores[q]) for q in order], dma_engine_mask=bits(eng),
-                                                  remote_sem=T.sem["rw"], srcs=[w], dsts=[w for q in order])],
-                               local_sem=T.sem["sent"])
-            g.wait_ge(T.sem["sent"], len(eng))
+            jobs = [("rp", n, [order[x] for x in range(3) if IDS[x] == k], "rh%d" % me, T.hin[:, me, :])] if k in IDS else []
+            for x, call in enumerate(PLAN):
+                mine = [(a, b, e) for (c, a, b), e in zip(call, deal(call, spare(topo, cores, me), eng)) if c == k]
+                if mine:
+                    jobs.append(("rq%d" % x, sum(len(e) for a, b, e in mine), order, "rw",
+                                 T.win[:, M * me + mine[0][0]:M * me + mine[-1][1]]))
+            for sem, cnt, to, rsem, w in jobs:
+                g.wait_ge(T.sem[sem], cnt)
+                g.remote_dma_fused([RemoteDMATransfer(dst_ids=[dst(topo, cores[q]) for q in to], dma_engine_mask=bits(eng),
+                                                      remote_sem=T.sem[rsem], srcs=[w], dsts=[w for q in to])],
+                                   local_sem=T.sem["sent"])
+            if jobs:
+                g.wait_ge(T.sem["sent"], len(jobs) * len(eng))
 
 
 def rank_program(g, core, T, topo):
@@ -107,7 +142,6 @@ def rank_program(g, core, T, topo):
     near = spare(topo, cores, me)
     nxt = (me + 1) % NR
     eng = topo.engines(core, cores[order[0]])
-    half = len(eng) // 2
     q_of = {"g": g, "v": g.vector, "a": g.scalar, "t": g.tensor, "s": g.sync}
     csem = {"g": "cg", "v": "cv", "a": "ca", "t": "ct"}
     total = {}
@@ -157,6 +191,12 @@ def rank_program(g, core, T, topo):
     def act(R, W, o, i):
         comp("a", R, W, lambda: g.scalar.activation(o, i, F.Copy))
 
+    def copy(q, R, W, o, i):
+        if q == "v":
+            V(R, W, lambda: g.vector.tensor_copy(o, i))
+        else:
+            act(R, W, o, i)
+
     def dma(q, out, in_, R, W):
         deps(q, R, W)
         s = "d%d" % ndma[0]
@@ -189,43 +229,57 @@ def rank_program(g, core, T, topo):
 
     dma("s", T.ht[:], T.tid[:], [], ["ht"])
     dma("a", T.lx[:], T.lett[:], [], ["lx"])
-    for h in range(2):
-        for x in range(8):
-            dma("sa"[x % 2], T.kx[:, h, x, :], T.kid[x, 16 * H * h:16 * H * (h + 1)], [], ["kx%d_%d" % (h, x)])
     dma("s", T.n1x[:], T.kid[:, 16:32], [], ["n1x"])
+    for h in range(len(AT) - 1):
+        for x in range(8):
+            dma(QS[h][x], T.kx[:, x, 16 * AT[h]:16 * AT[h + 1]], T.kid[x, 2048 * AT[h]:2048 * AT[h + 1]], [],
+                ["kx%d_%d" % (h, x)])
 
     def iota(key, out, pattern, base, mult):
         comp("g", [], [key], lambda: g.iota(out, pattern, base, mult, allow_small_or_imprecise_dtypes=True))
 
-    def equal(key, out, cols, x, y=None, R=()):
+    def select(key, out, R, in_, pattern, op, base, mult):
+        comp("g", R, [key], lambda: g.affine_select(out, in_, pattern, op, 0.0, base, mult))
+
+    def equal(key, out, x, y=None, R=()):
         if y is None:
-            V(["imk"] + list(R), [key], lambda: v.tensor_scalar(out, T.imk[:, 0:cols], x, None, A.is_equal))
+            V(["imk"] + list(R), [key], lambda: v.tensor_scalar(out, T.imk[:], x, None, A.is_equal))
         else:
-            V(["imk"] + list(R), [key], lambda: v.tensor_scalar(out, T.imk[:, 0:cols], x, y, A.is_equal, A.mult))
+            V(["imk"] + list(R), [key], lambda: v.tensor_scalar(out, T.imk[:], x, y, A.is_equal, A.mult))
 
     def zero(q):
         V([], ["tz%d" % q], lambda: v.memset(T.tw[:, M * q:M * q + M], 0.0))
 
-    iota("imk", T.imk[:], [[1, 143]], 0, -1)
+    iota("imk", T.imk[:], [[1, 128]], 0, -1)
     comp("g", [], ["pi"], lambda: g.iota(T.pi[:], [[1, 1]], 0, 1))
     comp("g", [], ["expi"], lambda: g.iota(T.expi[:], [[1, 4]], 4 * me, 0))
-    iota("one", T.one[:], [[0, 128]], 1, 0)
+    V([], ["one"], lambda: v.memset(T.one[:], 1.0))
+    select("e8", T.e8[0:8, :], ["one"], T.one[0:8, :], [[1, 8], [0, 16]], A.is_equal, 0, -1)
 
     zero(me)
-    act(["tz%d" % me], ["tz%d" % order[0]], T.tw[:, M * order[0]:M * order[0] + M], T.tw[:, M * me:M * me + M])
-    equal("ih", T.ih[:], 128, 0.0)
-    equal("ihn", T.ihn[:], 128, 0.0, -1.0)
-    equal("shb", T.shb[:], 128, 3.0)
+    act(["tz%d" % me], ["tza"], T.tw[:, M * order[1]:M * order[1] + ZA], T.tw[:, M * me:M * me + ZA])
+    equal("ib", T.ib[:], 0.0)
+    comp("a", ["ib"], ["i16"], lambda: g.scalar.activation(T.i16[:], T.ib[:], F.Copy, scale=16.0))
+    equal("ih", T.ih[:], 0.0)
+    equal("ihn", T.ihn[:], 0.0, -0.5)
+    equal("shb", T.shb[:], 3.0)
     V(["pi"], ["pci"], lambda: v.tensor_scalar(T.pci[:], T.pi[:], 15, None, A.bitwise_and))
     V(["expi"], ["expu"], lambda: v.tensor_copy(T.expu[:], T.expi[:]))
     V(["pci"], ["pcf"], lambda: v.tensor_copy(T.pcf[:], T.pci[:]))
-    zero(order[2])
+    V(["pi"], ["p4i"], lambda: v.tensor_scalar(T.p4i[:], T.pi[:], 3, None, A.bitwise_and))
+    V(["pci"], ["ncf"], lambda: v.tensor_scalar(T.ncf[:], T.pci[:], -1.0, None, A.mult))
+    V(["p4i"], ["p4f"], lambda: v.tensor_copy(T.p4f[:], T.p4i[:]))
+    iota("ai", T.ai[:], [[0, 8], [1, 4], [0, 4]], 0, 0)
 
+    copy(LFQ, ["lx"], ["lf"], lf, T.lx[:])
     act(["ht"], ["hb0"], T.hb[:, 0:48], T.ht[:])
     comp("a", ["ht"], ["hb2"], lambda: g.scalar.activation(T.hb[:, 96:144], T.ht[:], F.Sign))
-    act(["lx"], ["lf"], lf, T.lx[:])
     V(["ht", "hb0"], ["hb1"], lambda: v.tensor_tensor(T.hb[:, 48:96], T.ht[:], T.hb[:, 0:48], A.subtract))
-    send([(ranks, "rh%d" % me, eng, T.hb[:, 0:160], T.hin[:, me, :])], ["hb0", "hb1", "hb2", "lf"])
+    send([([cores[(me - 1) % NR]], "rx", eng, lcols(0, 8), T.hx[:])], ["lf"])
+    way = [([ranks[x] for x in range(3) if IDS[x] == SELF], "rh%d" % me, eng),
+           ([hs[k] for k in IO if k in IDS], "rp", near)]
+    send([w + (T.hb[:, 0:144], T.hin[:, me, :]) for w in way if w[0]], ["hb0", "hb1", "hb2"])
+    arrive("rx", len(eng), ["hx"])
     for q in others:
         arrive("rh%d" % q, len(eng), ["hin%d" % q])
     tws = {q: ["tw%d_%d" % (q, x) for x in range(3)] for q in range(NR)}
@@ -236,197 +290,242 @@ def rank_program(g, core, T, topo):
             i, R = (T.hb[:, 48 * x:48 * x + 48], ["hb%d" % x]) if q == me else (T.hin[:, q, 48 * x:48 * x + 48], ["hin%d" % q])
             dma("s", T.tw[x:128:16, M * q:M * q + M], i, R, [tws[q][x]])
 
-    planes(me)
     dma("s", T.lu[0:8, 0:1024], lf, ["lf"], ["lua"])
-    comp("g", ["one"], ["e8"], lambda: g.affine_select(T.e8[0:8, :], T.one[0:8, :], [[1, 8], [0, 16]], A.is_equal, 0.0, 0, -1))
-    comp("g", ["one"], ["sel"], lambda: g.affine_select(T.sel[:], T.one[:], [[16, 8], [0, 16]], A.is_equal, 0.0, 0, -1))
-
-    def cast(h):
-        R = ["kx%d_%d" % (h, x) for x in range(8)]
-        for j in range(3):
-            i = T.kx[:, h, :, 16 * j:16 * j + 16]
-            V(R, ["kc%d%d" % (h, j)], lambda: v.tensor_scalar(T.kc[:, h, j, :], i, LO, HI, A.max, A.min))
-            comp("a", R, ["kh%d%d" % (h, j)],
-                 lambda: g.scalar.activation(T.kh[:, h, j, :], i, F.Copy, bias=-float(H), scale=2.0))
-
-    def turn(h):
-        for j in range(3):
-            for s in range(2):
-                o = ps[2 * h + s][:, j:192:3]
-                comp("t", ["kc%d%d" % (h, j), "kh%d%d" % (h, j), "ih", "ihn"], ["ps%d" % (2 * h + s)],
-                     [lambda: pe.matmul(o, T.kh[:, h, j, :], T.ih[:, 64 * s:64 * s + 64], True, False),
-                      lambda: pe.matmul(o, T.kc[:, h, j, :], T.ihn[:, 64 * s:64 * s + 64], False, True)])
-
-    def leave(h):
-        a = M * me + H * h
-        V(["ps%d" % (2 * h)], ["w%da" % h], lambda: v.tensor_copy(T.win[:, a:a + 192], ps[2 * h][:, 0:192]))
-        act(["ps%d" % (2 * h + 1)], ["w%db" % h], T.win[:, a + 192:a + H], ps[2 * h + 1][:, 0:192])
-
-    own = ["w0a", "w0b", "w1a", "w1b"]
-
-    def go(ks):
-        n = len(near) // len(ks)
-        send([([hs[k]], "rq", near[n * x:n * x + n], quarter(T, me, k), quarter(T, me, k)) for x, k in enumerate(ks)],
-             [own[k] for k in ks])
-
-    blk = T.win[:, M * me:M * me + M]
-    tblk = T.tw[:, M * me:M * me + M]
-
-    cast(0)
-    turn(0)
-    V(["n1x"], ["n1u"], lambda: v.tensor_copy(T.n1u[:, 0:1], T.n1x[:]))
-    cast(1)
-    turn(1)
-    leave(0)
-    go([0, 1])
-    zero(order[1])
-    act(tws[me] + ["n1u"], ["g1"], T.g1[:], tblk.indirect(T.n1u[:, 0:1]))
-    act(["g1", "expu"], ["g1e"], T.g1e[:], T.g1[:].indirect(T.expu[:]))
-    comp("t", ["g1e", "shb"], ["ps4"], lambda: pe.matmul(ps[4][:, 0:64], T.shb[:], T.g1e[:], True, True))
-    leave(1)
-    go([2])
-    act(["ps4"], ["g1s"], T.g1s[:], ps[4][:, 0:64])
-
-    w1 = blk.indirect(T.n1u[:, 0:1])
-    V(own + ["n1u"], ["c2"], lambda: v.tensor_scalar(T.c2[:], w1, 256.0, -256.0, A.min, A.max))
-    V(own + ["n1u", "c2"], ["s2"], lambda: v.tensor_tensor(T.s2[:], w1, T.c2[:], A.add))
-    V(["s2"], ["n2u"], lambda: v.tensor_scalar(T.n2u[:], T.s2[:], 0.5, float(H), A.mult, A.add))
-    n2 = T.n2u[:, 4 * me:4 * me + 4]
-    nw, g12 = T.nw[:, 64 * me:64 * me + 64], T.g12[:, 64 * me:64 * me + 64]
-    act(own + ["n2u"], ["nw"], nw, blk.indirect(n2))
-    V(tws[me] + ["n2u", "g1s"], ["g12"], lambda: v.tensor_tensor(g12, tblk.indirect(n2), T.g1s[:], A.add))
-    send([(ranks, "rn", eng, nw, nw)], ["nw"])
-    send([(ranks, "rg", eng, g12, g12)], ["g12"])
-    send([(ranks, "rw", eng, quarter(T, me, 3), quarter(T, me, 3))], [own[3]])
-    arrive("rw", 4 * len(eng) * len(others), ["win"])
-    arrive("rn", len(eng) * len(others), ["nwin"])
-    arrive("rg", len(eng) * len(others), ["g12in"])
-
-    for q in order[::-1]:
-        planes(q)
-    tall = [k for q in range(NR) for k in tws[q]]
-
-    iota("vt", T.vt[:], [[0, 32]], 0, 0)
-
-    def weight(j, k, x, w):
-        i = T.vt[:, 8 * j:8 * k]
-        comp("g", ["vt"], ["vt"], lambda: g.affine_select(i, i, [[0, k - j], [-16, 8]], A.not_equal, w, -x, 1))
-
-    for x in range(2):
-        weight(0, 1, 3 + x, 1.0)
-        weight(1, 4, x, 1.0)
-    weight(0, 1, 5, K17)
-    for j in range(1, 4):
-        weight(j, j + 1, 2, (j + 1) * K17)
-    iota("onf", T.onf[:], [[0, 128]], 1, 0)
-    comp("g", ["onf"], ["id"], lambda: g.affine_select(T["id"][:], T.onf[:], [[1, 2], [2, 64]], A.is_equal, 0.0, 0, -1))
+    dma("s", T.le[0:127, :], T.hb[1:128, 144:152], ["lf"], ["le"])
+    planes(me)
+    dma("s", T.lu[0:8, 1024:1032], T.hx[0:128:16, :], ["hx"], ["lub"])
+    dma("s", T.le[15:128:16, :], T.hx[0:128:16, :], ["hx", "le"], ["le"])
 
     def letters(k):
         comp("t", ["lua", "e8"], ["ps%d" % (6 + k)],
              [lambda s=s: pe.matmul(ps[6 + k][:, s:512:8], T.e8[0:8, :], T.lu[0:8, 128 * s + 64 * k:128 * s + 64 * k + 64],
                                     True, True) for s in range(8)])
 
-    def mask(k):
-        V(["ps%d" % (6 + k), "pcf"], ["em%d" % k],
-          lambda: v.tensor_scalar(T.em[:, k:1024:2], ps[6 + k][:, 0:512], T.pcf[:], None, A.is_equal))
+    def cast(h):
+        R = ["kx%d_%d" % (h, x) for x in range(8)]
+        for j in range(AT[h], AT[h + 1]):
+            i = T.kx[:, :, 16 * j:16 * j + 16]
+            V(R, ["kc%d" % j], lambda: v.tensor_scalar(T.kc[:, j, :], i, LO, HI, A.max, A.min))
+            comp("a", R, ["kh%d" % j], lambda: g.scalar.activation(T.kh[:, j, :], i, F.Copy, bias=-H / 2.0))
+
+    def turn(h):
+        n = AT[h + 1] - AT[h]
+        for j in range(AT[h], AT[h + 1]):
+            for s in range(2):
+                o = ps[2 * h + s][:, j - AT[h]:64 * n:n]
+                comp("t", ["kc%d" % j, "kh%d" % j, "ih", "ihn"], ["ps%d" % (2 * h + s)],
+                     [lambda: pe.matmul(o, T.kh[:, j, :], T.ih[:, 64 * s:64 * s + 64], True, False),
+                      lambda: pe.matmul(o, T.kc[:, j, :], T.ihn[:, 64 * s:64 * s + 64], False, True)])
+
+    own = ["w%d" % k for k in range(2 * len(AT) - 2)]
+    cuts = [64 * (AT[k // 2] + AT[(k + 1) // 2]) for k in range(2 * len(AT) - 1)]
+
+    def leave(h):
+        for s in range(2):
+            k = 2 * h + s
+            copy("va"[s], ["ps%d" % k], [own[k]], T.win[:, M * me + cuts[k]:M * me + cuts[k + 1]],
+                 ps[k][:, 0:cuts[k + 1] - cuts[k]])
+
+    def go(h):
+        call = PLAN[h]
+        if call:
+            w = [T.win[:, M * me + a:M * me + b] for c, a, b in call]
+            send([((ranks, "rw") if c == SELF else ([hs[c]], "rq%d" % h)) + (e, i, i)
+                  for (c, a, b), e, i in zip(call, deal(call, near, eng), w)],
+                 [own[k] for k in range(len(own)) if any(a < cuts[k + 1] and cuts[k] < b for c, a, b in call)])
+
+    blk = T.win[:, M * me:M * me + M]
+    tblk = T.tw[:, M * me:M * me + M]
+
+    V(["n1x"], ["n1u"], lambda: v.tensor_copy(T.n1u[:, 0:1], T.n1x[:]))
+    cast(0)
+    turn(0)
+    for h in range(1, len(AT) - 1):
+        if h <= LF:
+            leave(h - 1)
+        cast(h)
+        turn(h)
+        if h > LF:
+            leave(h - 1)
+        go(h - 1)
+    leave(len(AT) - 2)
+    if not LATE:
+        go(len(AT) - 2)
+    act(tws[me] + ["n1u"], ["g1"], T.g1[:], tblk.indirect(T.n1u[:, 0:1]))
+    act(["g1", "expu"], ["g1e"], T.g1e[:], T.g1[:].indirect(T.expu[:]))
+    letters(1)
+    comp("t", ["g1e", "shb"], ["ps4"], lambda: pe.matmul(ps[4][:, 0:64], T.shb[:], T.g1e[:], True, True))
+
+    w1 = blk.indirect(T.n1u[:, 0:1])
+    V(own + ["n1u"], ["c2"], lambda: v.tensor_scalar(T.c2[:], w1, CL, -CL, A.min, A.max))
+    V(own + ["n1u"], ["s2"], lambda: v.tensor_scalar(T.s2[:], w1, float(H), None, A.add))
+    V(["s2", "c2"], ["n2u"], lambda: v.tensor_tensor(T.n2u[:], T.s2[:], T.c2[:], A.add))
+    n2 = T.n2u[:, 4 * me:4 * me + 4]
+    nw, g12 = T.nw[:, 64 * me:64 * me + 64], T.g12[:, 64 * me:64 * me + 64]
+    copy("v", own + ["n2u"], ["nw"], nw, blk.indirect(n2))
+    act(["ps4"], ["g1s"], T.g1s[:], ps[4][:, 0:64])
+    V(tws[me] + ["n2u", "g1s"], ["g12"], lambda: v.tensor_tensor(g12, tblk.indirect(n2), T.g1s[:], A.add))
+    if MERGE:
+        half = len(eng) // 2
+        send([(ranks, "rn", eng[:half], nw, nw), (ranks, "rg", eng[half:], g12, g12)], ["nw", "g12"])
+    else:
+        half = len(eng)
+        send([(ranks, "rn", eng, nw, nw)], ["nw"])
+        if LATE:
+            go(len(AT) - 2)
+        send([(ranks, "rg", eng, g12, g12)], ["g12"])
+    go(len(AT) - 1)
+    arrive("rw", sum(len(set(c for c, a, b in call)) for call in PLAN) * len(eng) * len(others), ["win"])
+    arrive("rn", half * len(others), ["nwin"])
+    arrive("rg", half * len(others), ["g12in"])
+
+    tall = [k for q in range(NR) for k in tws[q]]
+
+    select("g32", T.g32[:], ["one"], T.one[:, 0:32], [[-16, 8], [0, 4]], A.is_ge, 0, 1)
+    select("r32", T.r32[:], ["one"], T.one[:, 0:32], [[-4, 32]], A.is_ge, 0, 1)
+    select("g32", T.g32[:], ["g32"], T.g32[:], [[16, 8], [0, 4]], A.is_ge, 15, -1)
+    select("r32", T.r32[:], ["r32"], T.r32[:], [[4, 32]], A.is_ge, 3, -1)
+    select("wb", T.wb[:], ["one"], T.one[:, 0:16], [[3, 2], [-16, 8]], A.is_ge, -3, 1)
+    select("wb", T.wb[:], ["wb"], T.wb[:], [[-3, 2], [16, 8]], A.is_ge, 4, -1)
+    for j in range(4):
+        b = min(j, 1)
+        comp("g", ["wb"], ["vt%d" % j],
+             lambda: g.affine_select(T.vt[:, 8 * j:8 * j + 8], T.wb[:, 8 * b:8 * b + 8], [[-16, 8]], A.not_equal, (j + 1) * K17,
+                                     3 * b - 5, 1))
 
     letters(0)
-    letters(1)
-    equal("ib", T.ib[:], 128, 0.0)
-    V(["pcf"], ["zz"], lambda: v.tensor_scalar(T.zz[:], T.pcf[:], 0.0, None, A.is_equal))
-    V(["pcf"], ["nz"], lambda: v.tensor_scalar(T.nz[:], T.pcf[:], 0.0, None, A.not_equal))
-    V(["pcf"], ["k16"], lambda: v.tensor_scalar(T.k16[:], T.pcf[:], -1.0, 15.0, A.mult, A.add))
-    comp("a", ["ib"], ["i16"], lambda: g.scalar.activation(T.i16[:], T.ib[:], F.Copy, scale=16.0))
-    equal("sh", T.sh[:], 128, -1.0, T.nz[:], ["nz"])
-    equal("sh15", T.sh15[:], 128, 15.0, T.zz[:], ["zz"])
-    mask(0)
-    mask(1)
-    comp("t", ["lf", "hin%d" % nxt, "i16", "ib", "sh", "sh15"], ["ps5"],
+    comp("a", ["ps7", "ncf"], ["ab"], lambda: g.scalar.activation(T.ab[:], ps[7][:, 0:512], F.Abs, bias=T.ncf[:]))
+    comp("a", ["ab"], ["em1"], lambda: g.scalar.activation(T.em[:, 1:1024:2], T.ab[:], F.Relu, bias=1.0, scale=-1.0))
+    V(["ps6", "pcf"], ["em0"], lambda: v.tensor_scalar(T.em[:, 0:1024:2], ps[6][:, 0:512], T.pcf[:], None, A.is_equal))
+    comp("t", ["lf", "i16", "ib"], ["ps5"],
          [lambda: pe.matmul(ps[5][:, 0:63], T.i16[:], lcols(0, 63), True, False),
-          lambda: pe.matmul(ps[5][:, 0:63], T.ib[:], lcols(1, 64), False, True),
-          lambda: pe.matmul(ps[5][:, 63:64], T.i16[:], lcols(63, 64), True, False),
-          lambda: pe.matmul(ps[5][:, 63:64], T.sh[:], lcols(0, 1), False, False),
-          lambda: pe.matmul(ps[5][:, 63:64], T.sh15[:], T.hin[:, nxt, 144:145], False, True)])
-    comp("t", ["lua", "e8", "sel", "hin%d" % nxt], ["ps4"],
-         [lambda e=e: pe.matmul(ps[4][:, 16 * e:16 * e + 15], T.e8[0:8, :], T.lu[0:8, 64 + e:1024:64], True, True)
-          for e in range(3)]
-         + [lambda: pe.matmul(ps[4][:, 15:48:16], T.sel[:], T.hin[:, nxt, 144:147], True, True)])
-    act(["ps5"], ["cu"], T.cu[:], ps[5][:, 0:64])
-    V(["ps4", "pcf"], ["em2"], lambda: v.tensor_scalar(T.em[:, 1024:1072], ps[4][:, 0:48], T.pcf[:], None, A.is_equal))
-    equal("t1h", T.t1h[:], 143, T.k16[:], 0.5, ["k16"])
+          lambda: pe.matmul(ps[5][:, 0:63], T.ib[:], lcols(1, 64), False, True)])
+    copy("v", ["ps5"], ["cua"], T.cu[:, 0:63], ps[5][:, 0:63])
     V(["lx"], ["ow"], lambda: v.tensor_scalar(T.ow[:], T.lx[:], 2, None, A.arith_shift_right))
+    V(["ai", "p4f"], ["dm"], lambda: v.tensor_scalar(T.dm[:], T.ai[:], T.p4f[:], None, A.is_equal))
     V(["ow"], ["off"], lambda: v.tensor_scalar(T.off[:], T.ow[:], float(M), float(H), A.mult, A.add))
+    V(["tza"], ["tz%d" % order[1]], lambda: v.memset(T.tw[:, M * order[1] + ZA:M * order[1] + M], 0.0))
+    zero(order[2])
+    comp("a", own, ["tz%d" % order[0]],
+         lambda: g.scalar.activation(T.tw[:, M * order[0]:M * order[0] + M], blk, F.Copy, scale=0.0))
+    comp("t", ["lua", "lub", "e8", "lf", "le", "i16", "ib"], ["ps4"],
+         [lambda e=e: pe.matmul(ps[4][:, 16 * e:16 * e + 16], T.e8[0:8, :], T.lu[0:8, 64 + e:1032:64], True, True)
+          for e in range(3)]
+         + [lambda: pe.matmul(ps[4][:, 48:49], T.i16[:], lcols(63, 64), True, False),
+            lambda: pe.matmul(ps[4][:, 48:49], T.ib[:], T.le[:, 0:1], False, True)])
+    comp("a", ["ps4", "ncf"], ["ab2"], lambda: g.scalar.activation(T.ab2[:], ps[4][:, 0:48], F.Abs, bias=T.ncf[:]))
+    copy("a", ["ps4"], ["cub"], T.cu[:, 63:64], ps[4][:, 48:49])
+    comp("a", ["ab2"], ["em2"], lambda: g.scalar.activation(T.em[:, 1024:1072], T.ab2[:], F.Relu, bias=1.0, scale=-1.0))
+    act(["ib"], ["id"], T["id"][:], T.ib[:])
+    for q in (order[1], order[2], order[0]):
+        planes(q)
     ems = ["em0", "em1", "em2"]
+    cus = ["cua", "cub"]
 
-    portions = ((0, CUT), (CUT, 1024))
+    walked = {}
 
-    def walk(p, h, w, lst, e, R):
-        a, b = portions[h]
-        V(R + ems, ["%s%d" % (p, h)],
+    def walk(p, a, b, w, lst, e, R):
+        walked.setdefault((p, a // 512), []).append("%s_%d" % (p, a))
+        V(R + ems[:2 + (b + 16 * e > 1024)], ["%s_%d" % (p, a)],
           lambda: v.tensor_tensor(T[p][:, a:b], w.indirect(lst[:, a // 16:b // 16]), T.em[:, a + 16 * e:b + 16 * e], A.mult))
 
-    def nodes(bank, p, h):
-        a, b = portions[h]
-        comp("t", ["%s%d" % (p, h), "t1h"], ["ps%d" % bank],
-             [lambda i=i: pe.matmul(ps[bank][:, 0:(b - a) // 16], T.t1h[:, 15 - i:143 - i], T[p][:, a + i:b:16], i == 0,
-                                    i == 15) for i in range(16)])
+    def start(h):
+        comp("t", ["off", "ib"], ["ps%d" % (2 + h)],
+             lambda: pe.matmul(ps[2 + h][:, 0:32], T.ib[:], T.off[:, 32 * h:32 * h + 32], True, False))
 
-    def lists(bank, nm, h):
-        a, b = portions[h][0] // 16, portions[h][1] // 16
-        o = 64 * (nm == "n4u")
-        key = "%s%d" % (nm, h)
-        c, s, p = T.lc[:, o + a:o + b], T.ls[:, o + a:o + b], ps[bank][:, 0:b - a]
-        V(["ps%d" % bank], ["c" + key], lambda: v.tensor_scalar(c, p, 128.0, -128.0, A.min, A.max))
-        V(["ps%d" % bank, "off"], ["s" + key], lambda: v.tensor_tensor(s, p, T.off[:, a:b], A.add))
-        V(["c" + key, "s" + key], [key], lambda: v.tensor_tensor(T[nm][:, a:b], s, c, A.add))
+    def sums(p, h):
+        comp("t", walked[p, h] + ["g32"], ["ps%d" % h],
+             [lambda s=s: pe.matmul(ps[h][:, s:128:4], T[p][:, 512 * h + s:512 * h + 512:4], T.g32[:], True, True)
+              for s in range(4)])
+
+    def decode(h):
+        z, c = T.zb[:, h, :], T.zc[:, h, :]
+        V(["ps%d" % h, "dm"], ["z%d" % h], lambda: v.tensor_tensor(z, ps[h][:, 0:128], T.dm[:], A.mult))
+        V(["z%d" % h], ["c%d" % h], lambda: v.tensor_scalar(c, z, CL, -CL, A.min, A.max))
+
+    def back(h):
+        for k, x in (("z", T.zb), ("c", T.zc)):
+            comp("t", ["%s%d" % (k, h), "r32"], ["ps%d" % (2 + h)],
+                 lambda: pe.matmul(ps[2 + h][:, 0:32], x[:, h, :], T.r32[:], False, k == "c"))
+
+    def lists(q, nm, h):
+        copy(q, ["ps%d" % (2 + h)], ["%s%d" % (nm, h)], T[nm][:, 32 * h:32 * h + 32], ps[2 + h][:, 0:32])
 
     pieces = {"i12": [], "i3": [], "i4": []}
 
     def ids(q, rep, w, lst, a, b, R):
         key = "%s_%d" % (rep, a)
         pieces[rep].append(key)
-        i = w.indirect(lst[:, a // 16:b // 16])
-        if q == "v":
-            V(R, [key], lambda: v.tensor_copy(T[rep][:, a:b], i))
-        else:
-            act(R, [key], T[rep][:, a:b], i)
+        copy(q, R, [key], T[rep][:, a:b], w.indirect(lst[:, a // 16:b // 16]))
 
     def value(rep, bank, x, j):
-        comp("t", pieces[rep] + ["vt"], ["ps%d" % bank],
+        comp("t", pieces[rep] + ["vt%d" % k for k in range(j, j + x)], ["ps%d" % bank],
              [lambda s=s: pe.matmul(ps[bank][:, s:64 * x:8], T[rep][:, s:1024:8], T.vt[:, 8 * j:8 * j + 8 * x], True, True)
               for s in range(8)])
 
     win, twin = T.win[:, 0:3072], T.tw[:, 0:3072]
     for h in range(2):
-        walk("p3", h, T.nw[:, 0:256], T.cu, 2, ["nw", "nwin", "cu"])
-        nodes(h, "p3", h)
-    ids("a", "i12", T.g12[:, 0:256], T.cu, 0, 1024, ["g12", "g12in", "cu"])
+        start(h)
     for h in range(2):
-        lists(h, "n3u", h)
-        walk("p4", h, win, T.n3u, 3, own + ["win", "n3u%d" % h])
-        nodes(2 + h, "p4", h)
-        ids("a", "i3", twin, T.n3u, portions[h][0], portions[h][1], tall + ["n3u%d" % h])
+        walk("p3", 512 * h, 512 * h + 512, T.nw[:, 0:256], T.cu, 2, ["nw", "nwin"] + cus[:h + 1])
+        sums("p3", h)
+    ids("a", "i12", T.g12[:, 0:256], T.cu, 0, I12, ["g12", "g12in"] + cus)
+    for h in range(2):
+        decode(h)
+        back(h)
+    for h in range(2):
+        lists(L3[h], "n3u", h)
+    if I12 < 1024:
+        ids("a", "i12", T.g12[:, 0:256], T.cu, I12, 1024, ["g12", "g12in"] + cus)
+    for h in range(2):
+        start(h)
+    walk("p4", 0, 512, win, T.n3u, 3, own + ["win", "n3u0"])
     value("i12", 4, 2, 0)
-    value("i3", 5, 1, 2)
-    lists(2, "n4u", 0)
-    ids("v", "i4", twin, T.n4u, 0, CUT, tall + ["n4u0"])
-    lists(3, "n4u", 1)
-    ids("v", "i4", twin, T.n4u, CUT, IV, tall + ["n4u1"])
+    sums("p4", 0)
+    ids("a", "i3", twin, T.n3u, 0, 512, tall + ["n3u0"])
+    def best(slot):
+        if BP[0] == slot:
+            V(["ps4"], ["b1"], lambda: v.tensor_copy(T.b1[:], ps[4][:, 64:128]))
+        if BP[1] == slot:
+            V(["ps4", "b1"], ["b2"], lambda: v.tensor_tensor(T.b2[:], ps[4][:, 0:64], T.b1[:], A.max))
+        if BP[2] == slot:
+            V(["ps5", "b2"], ["b3"], lambda: v.tensor_tensor(T.b3[:], ps[5][:, 0:64], T.b2[:], A.max))
+
+    walk("p4", 512, P4, win, T.n3u, 3, own + ["win", "n3u1"])
+    ids("a", "i3", twin, T.n3u, 512, 1024, tall + ["n3u1"])
+    if P4 == 1024:
+        sums("p4", 1)
+    decode(0)
+    back(0)
+    if P4 < 1024:
+        walk("p4", P4, 1024, win, T.n3u, 3, own + ["win", "n3u1"])
+        sums("p4", 1)
+    lists("a", "n4u", 0)
+    if VP == 0:
+        value("i3", 5, 1, 2)
+    ids("a", "i4", twin, T.n4u, 0, 512, tall + ["n4u0"])
+    best(0)
+    decode(1)
+    back(1)
+    if VP == 1:
+        value("i3", 5, 1, 2)
+    best(1)
+    lists("v", "n4u", 1)
+    ids("v", "i4", twin, T.n4u, 512, IV, tall + ["n4u1"])
     ids("a", "i4", twin, T.n4u, IV, 1024, tall + ["n4u1"])
-    V(["ps4"], ["b1"], lambda: v.tensor_copy(T.b1[:], ps[4][:, 64:128]))
-    V(["ps4", "b1"], ["b2"], lambda: v.tensor_tensor(T.b2[:], ps[4][:, 0:64], T.b1[:], A.max))
     value("i4", 6, 1, 3)
-    V(["ps5", "b2"], ["b3"], lambda: v.tensor_tensor(T.b3[:], ps[5][:, 0:64], T.b2[:], A.max))
+    best(2)
     V(["ps6", "b3"], ["res"], lambda: v.tensor_tensor(T.res[:], ps[6][:, 0:64], T.b3[:], A.max))
 
-    p = ps[7][0:64, 0:128]
-    comp("t", ["res", "id"], ["ps7"], lambda: pe.matmul(p, T.res[:], T["id"][:], True, True))
-    V(["ps7"], ["rt"], lambda: v.tensor_scalar(T.rt[0:64, :], p, RND, RND, A.add, A.subtract))
-    V(["ps7", "rt"], ["yi"], lambda: v.tensor_tensor(T.yi[0:64, :], p, T.rt[0:64, :], A.subtract))
-    comp("a", ["rt"], ["yl"], lambda: g.scalar.activation(T.yl[0:64, :], T.rt[0:64, :], F.Copy, scale=1.0 / K17))
+    half = [slice(64 * hi, 64 * hi + 64) for hi in range(2)]
+    comp("t", ["res", "id"], ["ps7"], [lambda hi=hi: pe.matmul(ps[7][half[hi], 0:64], T.res[:], T["id"][:, hi:128:2], True, True) for hi in range(2)])
+    p = ps[7][:, 0:64]
+    V(["ps7"], ["rt"], lambda: v.tensor_scalar(T.rt[:], p, RND, RND, A.add, A.subtract))
+    V(["ps7", "rt"], ["yi"], lambda: v.tensor_tensor(T.yi[:], p, T.rt[:], A.subtract))
+    comp("a", ["rt"], ["yl"], lambda: g.scalar.activation(T.yl[:], T.rt[:], F.Copy, scale=1.0 / K17))
     for hi in range(2):
-        dma("s", T.yid[:, 512 * hi:512 * hi + 512], T.yi[0:64, 64 * hi:64 * hi + 64], ["yi"], ["oi%d" % hi])
-        dma("a", T.ylen[:, 512 * hi:512 * hi + 512], T.yl[0:64, 64 * hi:64 * hi + 64], ["yl"], ["ol%d" % hi])
+        dma("s", T.yid[:, 512 * hi:512 * hi + 512], T.yi[half[hi], :], ["yi"], ["oi%d" % hi])
+        dma("a", T.ylen[:, 512 * hi:512 * hi + 512], T.yl[half[hi], :], ["yl"], ["ol%d" % hi])
 
     for s in total:
         if seen.get(s, 0) < total[s]:

import numpy as np
from concourse.bass import DstId, RemoteDMATransfer
from concourse.mybir import AluOpType as A, ActivationFunctionType as F

NR = 4
M = 768
H = 384
LO, HI = 128.0, 640.0
CL = 128.0
P4 = 1024
AT = [0, 3, 6]
QS = ["asasasas"] * 3
IO = (0, 1, 2)
LFQ = "v"
L3 = "aa"
BP = (1, 2, 2)
VP = 1
I12 = 1024
LATE = False
ZA = 256
LF = 0
SELF = -1
IDS = [0, 1, 2]
PLAN = [[(SELF, 0, 160), (0, 160, 320)], [(1, 320, 480), (2, 480, 640)], [(SELF, 640, 768)]]
MERGE = False
IV = 928
K17 = 131072.0
RND = 12582912.0 * K17
HF = "float16"
BF = "bfloat16"
F32 = "float32"
I32 = "int32"
U16 = "uint16"


def sb(cols, dtype):
    return ("sbuf", [128] + (cols if isinstance(cols, list) else [cols]), dtype)


SCRATCH = {
    "lx": sb(64, I32), "ht": sb(48, I32), "n1x": sb(1, I32), "hb": sb(208, BF), "hin": sb([4, 144], BF),
    "hx": sb(8, BF), "le": sb(8, BF), "ab": sb(512, BF), "ab2": sb(48, BF), "ncf": sb(1, F32),
    "kx": sb([8, 96], I32), "kh": sb([6, 128], HF), "kc": sb([6, 128], HF),
    "win": sb(3072, BF), "tw": sb(3072, BF), "nw": sb(256, BF), "g12": sb(256, BF),
    "lu": sb(1032, BF), "em": sb(1072, BF),
    "pi": sb(1, I32), "pci": sb(1, I32), "pcf": sb(1, F32), "zz": sb(1, F32), "nz": sb(1, F32),
    "imk": sb(128, BF), "one": sb(128, BF), "wb": sb(16, BF),
    "expi": sb(4, I32), "expu": sb(4, U16),
    "e8": sb(128, BF), "ih": sb(128, HF), "ihn": sb(128, HF), "ib": sb(128, BF), "i16": sb(128, BF),
    "sh": sb(128, BF), "sh15": sb(128, BF), "shb": sb(128, BF), "vt": sb(32, BF), "id": sb(128, F32),
    "ow": sb(64, I32), "off": sb(64, BF),
    "cu": sb(64, U16), "n1u": sb(2, U16), "n2u": sb(16, U16), "n3u": sb(64, U16), "n4u": sb(64, U16),
    "c2": sb(16, F32), "s2": sb(16, F32), "zb": sb([2, 128], BF), "zc": sb([2, 128], BF),
    "g32": sb(32, BF), "r32": sb(32, BF), "ai": sb(128, BF), "dm": sb(128, BF), "p4i": sb(1, I32), "p4f": sb(1, F32),
    "p3": sb(1024, BF), "p4": sb(1024, BF),
    "g1": sb(16, BF), "g1e": sb(64, BF), "g1s": sb(64, BF),
    "i12": sb(1024, BF), "i3": sb(1024, BF), "i4": sb(1024, BF),
    "b1": sb(64, F32), "b2": sb(64, F32), "b3": sb(64, F32),
    "res": sb(64, F32), "rt": sb(64, F32), "yl": sb(64, F32), "yi": sb(64, F32),
}
for _i in range(8):
    SCRATCH["ps%d" % _i] = ("psum", [128, 512], F32)
SEMAPHORES = (["cv", "ca", "ct", "cg", "sent", "rw", "rn", "rg", "rq0", "rq1", "rq2", "rq3", "rp", "rx"] + ["rh%d" % i for i in range(NR)]
              + ["d%d" % i for i in range(48)])


def bits(engines):
    return sum(1 << e for e in engines)


def far_first(topo, cores, me):
    chip = topo.chip(cores[me])
    others = [q for q in range(NR) if q != me]
    mate = [q for q in others if topo.mates(chip, topo.chip(cores[q]))]
    plane = [q for q in others if topo.same_plane(chip, topo.chip(cores[q]))]
    return [q for q in others if q not in mate + plane] + plane + mate


def helpers(topo, cores, me):
    core = cores[me]
    able = [c for c in topo.cores_of(core) if c != core and all(topo.may_write(c, d) for d in cores if d != core)]
    return sorted(able, key=lambda c: topo.die(c) == topo.die(core))


def dst(topo, d):
    rid, pid, _ = topo.addr(d)
    return DstId(rid=rid, pnc=pid)


def spare(topo, cores, me):
    off = topo.engines(cores[me], cores[(me + 1) % NR])
    return [e for e in topo.engines(cores[me], helpers(topo, cores, me)[0]) if e not in off]


def deal(call, near, eng):
    k = len([c for c, a, b in call if c != SELF])
    share = {0: [], 1: [1], 2: [2, 2], 3: [2, 4, 4], 4: [4, 4, 4, 4]}[k]
    out, at = [], 0
    for c, a, b in call:
        if c == SELF:
            out.append(eng)
        else:
            n = len(near) // share.pop(0)
            out.append(near[at:at + n])
            at += n
    return out


def hand_on(g, core, T, topo):
    cores = list(T.cores)
    for me in range(NR):
        hs = helpers(topo, cores, me)
        if core in hs:
            k = hs.index(core)
            n = len(spare(topo, cores, me))
            order = far_first(topo, cores, me)
            eng = topo.engines(core, cores[order[0]])
            jobs = [("rp", n, [order[x] for x in range(3) if IDS[x] == k], "rh%d" % me, T.hin[:, me, :])] if k in IDS else []
            for x, call in enumerate(PLAN):
                mine = [(a, b, e) for (c, a, b), e in zip(call, deal(call, spare(topo, cores, me), eng)) if c == k]
                if mine:
                    jobs.append(("rq%d" % x, sum(len(e) for a, b, e in mine), order, "rw",
                                 T.win[:, M * me + mine[0][0]:M * me + mine[-1][1]]))
            for sem, cnt, to, rsem, w in jobs:
                g.wait_ge(T.sem[sem], cnt)
                g.remote_dma_fused([RemoteDMATransfer(dst_ids=[dst(topo, cores[q]) for q in to], dma_engine_mask=bits(eng),
                                                      remote_sem=T.sem[rsem], srcs=[w], dsts=[w for q in to])],
                                   local_sem=T.sem["sent"])
            if jobs:
                g.wait_ge(T.sem["sent"], len(jobs) * len(eng))


def rank_program(g, core, T, topo):
    me = T.rank_of(core)
    if me is None:
        hand_on(g, core, T, topo)
        return
    cores = list(T.cores)
    others = [q for q in range(NR) if q != me]
    order = far_first(topo, cores, me)
    hs = helpers(topo, cores, me)
    near = spare(topo, cores, me)
    nxt = (me + 1) % NR
    eng = topo.engines(core, cores[order[0]])
    q_of = {"g": g, "v": g.vector, "a": g.scalar, "t": g.tensor, "s": g.sync}
    csem = {"g": "cg", "v": "cv", "a": "ca", "t": "ct"}
    total = {}
    waited = {}
    seen = {}
    lastw = {}
    reads = {}
    ndma = [0]

    def wait(q, evs):
        most = {}
        for s, x in evs:
            most[s] = max(x, most.get(s, 0))
        for s in most:
            if waited.get((q, s), 0) < most[s]:
                q_of[q].wait_ge(T.sem[s], most[s])
                waited[(q, s)] = most[s]
                seen[s] = max(seen.get(s, 0), most[s])

    def deps(q, R, W):
        own = csem.get(q)
        evs = []
        for k in R:
            evs += lastw[k]
        for k in W:
            evs += [e for e in lastw.get(k, []) + reads.get(k, []) if e[0] != own]
        wait(q, evs)

    def note(ev, R, W):
        for k in W:
            lastw[k] = [ev]
            reads[k] = []
        for k in R:
            reads.setdefault(k, []).append(ev)

    def comp(q, R, W, calls):
        deps(q, R, W)
        s = csem[q]
        for c in (calls if isinstance(calls, list) else [calls]):
            c().then_inc(T.sem[s], 1)
            total[s] = total.get(s, 0) + 1
        note((s, total[s]), R, W)

    def V(R, W, *calls):
        comp("v", R, W, list(calls))

    def act(R, W, o, i):
        comp("a", R, W, lambda: g.scalar.activation(o, i, F.Copy))

    def copy(q, R, W, o, i):
        if q == "v":
            V(R, W, lambda: g.vector.tensor_copy(o, i))
        else:
            act(R, W, o, i)

    def dma(q, out, in_, R, W):
        deps(q, R, W)
        s = "d%d" % ndma[0]
        ndma[0] += 1
        q_of[q].dma_start(out, in_).then_inc(T.sem[s], 16)
        total[s] = 16
        note((s, 16), R, W)

    def arrive(s, x, keys):
        total[s] = total.get(s, 0) + x
        for k in keys:
            lastw[k] = [(s, total[s])]

    ranks = [cores[q] for q in order]

    def send(pieces, R):
        deps("g", R, [])
        tr = [RemoteDMATransfer(dst_ids=[dst(topo, c) for c in to], dma_engine_mask=bits(e), remote_sem=T.sem[s],
                                srcs=[i], dsts=[o for c in to]) for to, s, e, i, o in pieces]
        g.remote_dma_fused(tr, local_sem=T.sem["sent"])
        total["sent"] = total.get("sent", 0) + sum(len(x[2]) for x in pieces)

    v = g.vector
    pe = g.tensor
    ps = [T["ps%d" % i] for i in range(8)]
    lf = T.hb[:, 144:208]

    def lcols(a, b):
        return T.hb[:, 144 + a:144 + b]

    dma("s", T.ht[:], T.tid[:], [], ["ht"])
    dma("a", T.lx[:], T.lett[:], [], ["lx"])
    dma("s", T.n1x[:], T.kid[:, 16:32], [], ["n1x"])
    for h in range(len(AT) - 1):
        for x in range(8):
            dma(QS[h][x], T.kx[:, x, 16 * AT[h]:16 * AT[h + 1]], T.kid[x, 2048 * AT[h]:2048 * AT[h + 1]], [],
                ["kx%d_%d" % (h, x)])

    def iota(key, out, pattern, base, mult):
        comp("g", [], [key], lambda: g.iota(out, pattern, base, mult, allow_small_or_imprecise_dtypes=True))

    def select(key, out, R, in_, pattern, op, base, mult):
        comp("g", R, [key], lambda: g.affine_select(out, in_, pattern, op, 0.0, base, mult))

    def equal(key, out, x, y=None, R=()):
        if y is None:
            V(["imk"] + list(R), [key], lambda: v.tensor_scalar(out, T.imk[:], x, None, A.is_equal))
        else:
            V(["imk"] + list(R), [key], lambda: v.tensor_scalar(out, T.imk[:], x, y, A.is_equal, A.mult))

    def zero(q):
        V([], ["tz%d" % q], lambda: v.memset(T.tw[:, M * q:M * q + M], 0.0))

    iota("imk", T.imk[:], [[1, 128]], 0, -1)
    comp("g", [], ["pi"], lambda: g.iota(T.pi[:], [[1, 1]], 0, 1))
    comp("g", [], ["expi"], lambda: g.iota(T.expi[:], [[1, 4]], 4 * me, 0))
    V([], ["one"], lambda: v.memset(T.one[:], 1.0))
    select("e8", T.e8[0:8, :], ["one"], T.one[0:8, :], [[1, 8], [0, 16]], A.is_equal, 0, -1)

    zero(me)
    act(["tz%d" % me], ["tza"], T.tw[:, M * order[1]:M * order[1] + ZA], T.tw[:, M * me:M * me + ZA])
    equal("ib", T.ib[:], 0.0)
    comp("a", ["ib"], ["i16"], lambda: g.scalar.activation(T.i16[:], T.ib[:], F.Copy, scale=16.0))
    equal("ih", T.ih[:], 0.0)
    equal("ihn", T.ihn[:], 0.0, -0.5)
    equal("shb", T.shb[:], 3.0)
    V(["pi"], ["pci"], lambda: v.tensor_scalar(T.pci[:], T.pi[:], 15, None, A.bitwise_and))
    V(["expi"], ["expu"], lambda: v.tensor_copy(T.expu[:], T.expi[:]))
    V(["pci"], ["pcf"], lambda: v.tensor_copy(T.pcf[:], T.pci[:]))
    V(["pi"], ["p4i"], lambda: v.tensor_scalar(T.p4i[:], T.pi[:], 3, None, A.bitwise_and))
    V(["pci"], ["ncf"], lambda: v.tensor_scalar(T.ncf[:], T.pci[:], -1.0, None, A.mult))
    V(["p4i"], ["p4f"], lambda: v.tensor_copy(T.p4f[:], T.p4i[:]))
    iota("ai", T.ai[:], [[0, 8], [1, 4], [0, 4]], 0, 0)

    copy(LFQ, ["lx"], ["lf"], lf, T.lx[:])
    act(["ht"], ["hb0"], T.hb[:, 0:48], T.ht[:])
    comp("a", ["ht"], ["hb2"], lambda: g.scalar.activation(T.hb[:, 96:144], T.ht[:], F.Sign))
    V(["ht", "hb0"], ["hb1"], lambda: v.tensor_tensor(T.hb[:, 48:96], T.ht[:], T.hb[:, 0:48], A.subtract))
    send([([cores[(me - 1) % NR]], "rx", eng, lcols(0, 8), T.hx[:])], ["lf"])
    way = [([ranks[x] for x in range(3) if IDS[x] == SELF], "rh%d" % me, eng),
           ([hs[k] for k in IO if k in IDS], "rp", near)]
    send([w + (T.hb[:, 0:144], T.hin[:, me, :]) for w in way if w[0]], ["hb0", "hb1", "hb2"])
    arrive("rx", len(eng), ["hx"])
    for q in others:
        arrive("rh%d" % q, len(eng), ["hin%d" % q])
    tws = {q: ["tw%d_%d" % (q, x) for x in range(3)] for q in range(NR)}

    def planes(q):
        for x in (0, 2, 1):
            deps("s", ["tz%d" % q], [])
            i, R = (T.hb[:, 48 * x:48 * x + 48], ["hb%d" % x]) if q == me else (T.hin[:, q, 48 * x:48 * x + 48], ["hin%d" % q])
            dma("s", T.tw[x:128:16, M * q:M * q + M], i, R, [tws[q][x]])

    dma("s", T.lu[0:8, 0:1024], lf, ["lf"], ["lua"])
    dma("s", T.le[0:127, :], T.hb[1:128, 144:152], ["lf"], ["le"])
    planes(me)
    dma("s", T.lu[0:8, 1024:1032], T.hx[0:128:16, :], ["hx"], ["lub"])
    dma("s", T.le[15:128:16, :], T.hx[0:128:16, :], ["hx", "le"], ["le"])

    def letters(k):
        comp("t", ["lua", "e8"], ["ps%d" % (6 + k)],
             [lambda s=s: pe.matmul(ps[6 + k][:, s:512:8], T.e8[0:8, :], T.lu[0:8, 128 * s + 64 * k:128 * s + 64 * k + 64],
                                    True, True) for s in range(8)])

    def cast(h):
        R = ["kx%d_%d" % (h, x) for x in range(8)]
        for j in range(AT[h], AT[h + 1]):
            i = T.kx[:, :, 16 * j:16 * j + 16]
            V(R, ["kc%d" % j], lambda: v.tensor_scalar(T.kc[:, j, :], i, LO, HI, A.max, A.min))
            comp("a", R, ["kh%d" % j], lambda: g.scalar.activation(T.kh[:, j, :], i, F.Copy, bias=-H / 2.0))

    def turn(h):
        n = AT[h + 1] - AT[h]
        for j in range(AT[h], AT[h + 1]):
            for s in range(2):
                o = ps[2 * h + s][:, j - AT[h]:64 * n:n]
                comp("t", ["kc%d" % j, "kh%d" % j, "ih", "ihn"], ["ps%d" % (2 * h + s)],
                     [lambda: pe.matmul(o, T.kh[:, j, :], T.ih[:, 64 * s:64 * s + 64], True, False),
                      lambda: pe.matmul(o, T.kc[:, j, :], T.ihn[:, 64 * s:64 * s + 64], False, True)])

    own = ["w%d" % k for k in range(2 * len(AT) - 2)]
    cuts = [64 * (AT[k // 2] + AT[(k + 1) // 2]) for k in range(2 * len(AT) - 1)]

    def leave(h):
        for s in range(2):
            k = 2 * h + s
            copy("va"[s], ["ps%d" % k], [own[k]], T.win[:, M * me + cuts[k]:M * me + cuts[k + 1]],
                 ps[k][:, 0:cuts[k + 1] - cuts[k]])

    def go(h):
        call = PLAN[h]
        if call:
            w = [T.win[:, M * me + a:M * me + b] for c, a, b in call]
            send([((ranks, "rw") if c == SELF else ([hs[c]], "rq%d" % h)) + (e, i, i)
                  for (c, a, b), e, i in zip(call, deal(call, near, eng), w)],
                 [own[k] for k in range(len(own)) if any(a < cuts[k + 1] and cuts[k] < b for c, a, b in call)])

    blk = T.win[:, M * me:M * me + M]
    tblk = T.tw[:, M * me:M * me + M]

    V(["n1x"], ["n1u"], lambda: v.tensor_copy(T.n1u[:, 0:1], T.n1x[:]))
    cast(0)
    turn(0)
    for h in range(1, len(AT) - 1):
        if h <= LF:
            leave(h - 1)
        cast(h)
        turn(h)
        if h > LF:
            leave(h - 1)
        go(h - 1)
    leave(len(AT) - 2)
    if not LATE:
        go(len(AT) - 2)
    act(tws[me] + ["n1u"], ["g1"], T.g1[:], tblk.indirect(T.n1u[:, 0:1]))
    act(["g1", "expu"], ["g1e"], T.g1e[:], T.g1[:].indirect(T.expu[:]))
    letters(1)
    comp("t", ["g1e", "shb"], ["ps4"], lambda: pe.matmul(ps[4][:, 0:64], T.shb[:], T.g1e[:], True, True))

    w1 = blk.indirect(T.n1u[:, 0:1])
    V(own + ["n1u"], ["c2"], lambda: v.tensor_scalar(T.c2[:], w1, CL, -CL, A.min, A.max))
    V(own + ["n1u"], ["s2"], lambda: v.tensor_scalar(T.s2[:], w1, float(H), None, A.add))
    V(["s2", "c2"], ["n2u"], lambda: v.tensor_tensor(T.n2u[:], T.s2[:], T.c2[:], A.add))
    n2 = T.n2u[:, 4 * me:4 * me + 4]
    nw, g12 = T.nw[:, 64 * me:64 * me + 64], T.g12[:, 64 * me:64 * me + 64]
    copy("v", own + ["n2u"], ["nw"], nw, blk.indirect(n2))
    act(["ps4"], ["g1s"], T.g1s[:], ps[4][:, 0:64])
    V(tws[me] + ["n2u", "g1s"], ["g12"], lambda: v.tensor_tensor(g12, tblk.indirect(n2), T.g1s[:], A.add))
    if MERGE:
        half = len(eng) // 2
        send([(ranks, "rn", eng[:half], nw, nw), (ranks, "rg", eng[half:], g12, g12)], ["nw", "g12"])
    else:
        half = len(eng)
        send([(ranks, "rn", eng, nw, nw)], ["nw"])
        if LATE:
            go(len(AT) - 2)
        send([(ranks, "rg", eng, g12, g12)], ["g12"])
    go(len(AT) - 1)
    arrive("rw", sum(len(set(c for c, a, b in call)) for call in PLAN) * len(eng) * len(others), ["win"])
    arrive("rn", half * len(others), ["nwin"])
    arrive("rg", half * len(others), ["g12in"])

    tall = [k for q in range(NR) for k in tws[q]]

    select("g32", T.g32[:], ["one"], T.one[:, 0:32], [[-16, 8], [0, 4]], A.is_ge, 0, 1)
    select("r32", T.r32[:], ["one"], T.one[:, 0:32], [[-4, 32]], A.is_ge, 0, 1)
    select("g32", T.g32[:], ["g32"], T.g32[:], [[16, 8], [0, 4]], A.is_ge, 15, -1)
    select("r32", T.r32[:], ["r32"], T.r32[:], [[4, 32]], A.is_ge, 3, -1)
    select("wb", T.wb[:], ["one"], T.one[:, 0:16], [[3, 2], [-16, 8]], A.is_ge, -3, 1)
    select("wb", T.wb[:], ["wb"], T.wb[:], [[-3, 2], [16, 8]], A.is_ge, 4, -1)
    for j in range(4):
        b = min(j, 1)
        comp("g", ["wb"], ["vt%d" % j],
             lambda: g.affine_select(T.vt[:, 8 * j:8 * j + 8], T.wb[:, 8 * b:8 * b + 8], [[-16, 8]], A.not_equal, (j + 1) * K17,
                                     3 * b - 5, 1))

    letters(0)
    comp("a", ["ps7", "ncf"], ["ab"], lambda: g.scalar.activation(T.ab[:], ps[7][:, 0:512], F.Abs, bias=T.ncf[:]))
    comp("a", ["ab"], ["em1"], lambda: g.scalar.activation(T.em[:, 1:1024:2], T.ab[:], F.Relu, bias=1.0, scale=-1.0))
    V(["ps6", "pcf"], ["em0"], lambda: v.tensor_scalar(T.em[:, 0:1024:2], ps[6][:, 0:512], T.pcf[:], None, A.is_equal))
    comp("t", ["lf", "i16", "ib"], ["ps5"],
         [lambda: pe.matmul(ps[5][:, 0:63], T.i16[:], lcols(0, 63), True, False),
          lambda: pe.matmul(ps[5][:, 0:63], T.ib[:], lcols(1, 64), False, True)])
    copy("v", ["ps5"], ["cua"], T.cu[:, 0:63], ps[5][:, 0:63])
    V(["lx"], ["ow"], lambda: v.tensor_scalar(T.ow[:], T.lx[:], 2, None, A.arith_shift_right))
    V(["ai", "p4f"], ["dm"], lambda: v.tensor_scalar(T.dm[:], T.ai[:], T.p4f[:], None, A.is_equal))
    V(["ow"], ["off"], lambda: v.tensor_scalar(T.off[:], T.ow[:], float(M), float(H), A.mult, A.add))
    V(["tza"], ["tz%d" % order[1]], lambda: v.memset(T.tw[:, M * order[1] + ZA:M * order[1] + M], 0.0))
    zero(order[2])
    comp("a", own, ["tz%d" % order[0]],
         lambda: g.scalar.activation(T.tw[:, M * order[0]:M * order[0] + M], blk, F.Copy, scale=0.0))
    comp("t", ["lua", "lub", "e8", "lf", "le", "i16", "ib"], ["ps4"],
         [lambda e=e: pe.matmul(ps[4][:, 16 * e:16 * e + 16], T.e8[0:8, :], T.lu[0:8, 64 + e:1032:64], True, True)
          for e in range(3)]
         + [lambda: pe.matmul(ps[4][:, 48:49], T.i16[:], lcols(63, 64), True, False),
            lambda: pe.matmul(ps[4][:, 48:49], T.ib[:], T.le[:, 0:1], False, True)])
    comp("a", ["ps4", "ncf"], ["ab2"], lambda: g.scalar.activation(T.ab2[:], ps[4][:, 0:48], F.Abs, bias=T.ncf[:]))
    copy("a", ["ps4"], ["cub"], T.cu[:, 63:64], ps[4][:, 48:49])
    comp("a", ["ab2"], ["em2"], lambda: g.scalar.activation(T.em[:, 1024:1072], T.ab2[:], F.Relu, bias=1.0, scale=-1.0))
    act(["ib"], ["id"], T["id"][:], T.ib[:])
    for q in (order[1], order[2], order[0]):
        planes(q)
    ems = ["em0", "em1", "em2"]
    cus = ["cua", "cub"]

    walked = {}

    def walk(p, a, b, w, lst, e, R):
        walked.setdefault((p, a // 512), []).append("%s_%d" % (p, a))
        V(R + ems[:2 + (b + 16 * e > 1024)], ["%s_%d" % (p, a)],
          lambda: v.tensor_tensor(T[p][:, a:b], w.indirect(lst[:, a // 16:b // 16]), T.em[:, a + 16 * e:b + 16 * e], A.mult))

    def start(h):
        comp("t", ["off", "ib"], ["ps%d" % (2 + h)],
             lambda: pe.matmul(ps[2 + h][:, 0:32], T.ib[:], T.off[:, 32 * h:32 * h + 32], True, False))

    def sums(p, h):
        comp("t", walked[p, h] + ["g32"], ["ps%d" % h],
             [lambda s=s: pe.matmul(ps[h][:, s:128:4], T[p][:, 512 * h + s:512 * h + 512:4], T.g32[:], True, True)
              for s in range(4)])

    def decode(h):
        z, c = T.zb[:, h, :], T.zc[:, h, :]
        V(["ps%d" % h, "dm"], ["z%d" % h], lambda: v.tensor_tensor(z, ps[h][:, 0:128], T.dm[:], A.mult))
        V(["z%d" % h], ["c%d" % h], lambda: v.tensor_scalar(c, z, CL, -CL, A.min, A.max))

    def back(h):
        for k, x in (("z", T.zb), ("c", T.zc)):
            comp("t", ["%s%d" % (k, h), "r32"], ["ps%d" % (2 + h)],
                 lambda: pe.matmul(ps[2 + h][:, 0:32], x[:, h, :], T.r32[:], False, k == "c"))

    def lists(q, nm, h):
        copy(q, ["ps%d" % (2 + h)], ["%s%d" % (nm, h)], T[nm][:, 32 * h:32 * h + 32], ps[2 + h][:, 0:32])

    pieces = {"i12": [], "i3": [], "i4": []}

    def ids(q, rep, w, lst, a, b, R):
        key = "%s_%d" % (rep, a)
        pieces[rep].append(key)
        copy(q, R, [key], T[rep][:, a:b], w.indirect(lst[:, a // 16:b // 16]))

    def value(rep, bank, x, j):
        comp("t", pieces[rep] + ["vt%d" % k for k in range(j, j + x)], ["ps%d" % bank],
             [lambda s=s: pe.matmul(ps[bank][:, s:64 * x:8], T[rep][:, s:1024:8], T.vt[:, 8 * j:8 * j + 8 * x], True, True)
              for s in range(8)])

    win, twin = T.win[:, 0:3072], T.tw[:, 0:3072]
    for h in range(2):
        start(h)
    for h in range(2):
        walk("p3", 512 * h, 512 * h + 512, T.nw[:, 0:256], T.cu, 2, ["nw", "nwin"] + cus[:h + 1])
        sums("p3", h)
    ids("a", "i12", T.g12[:, 0:256], T.cu, 0, I12, ["g12", "g12in"] + cus)
    for h in range(2):
        decode(h)
        back(h)
    for h in range(2):
        lists(L3[h], "n3u", h)
    if I12 < 1024:
        ids("a", "i12", T.g12[:, 0:256], T.cu, I12, 1024, ["g12", "g12in"] + cus)
    for h in range(2):
        start(h)
    walk("p4", 0, 512, win, T.n3u, 3, own + ["win", "n3u0"])
    value("i12", 4, 2, 0)
    sums("p4", 0)
    ids("a", "i3", twin, T.n3u, 0, 512, tall + ["n3u0"])
    def best(slot):
        if BP[0] == slot:
            V(["ps4"], ["b1"], lambda: v.tensor_copy(T.b1[:], ps[4][:, 64:128]))
        if BP[1] == slot:
            V(["ps4", "b1"], ["b2"], lambda: v.tensor_tensor(T.b2[:], ps[4][:, 0:64], T.b1[:], A.max))
        if BP[2] == slot:
            V(["ps5", "b2"], ["b3"], lambda: v.tensor_tensor(T.b3[:], ps[5][:, 0:64], T.b2[:], A.max))

    walk("p4", 512, P4, win, T.n3u, 3, own + ["win", "n3u1"])
    ids("a", "i3", twin, T.n3u, 512, 1024, tall + ["n3u1"])
    if P4 == 1024:
        sums("p4", 1)
    decode(0)
    back(0)
    if P4 < 1024:
        walk("p4", P4, 1024, win, T.n3u, 3, own + ["win", "n3u1"])
        sums("p4", 1)
    lists("a", "n4u", 0)
    if VP == 0:
        value("i3", 5, 1, 2)
    ids("a", "i4", twin, T.n4u, 0, 512, tall + ["n4u0"])
    best(0)
    decode(1)
    back(1)
    if VP == 1:
        value("i3", 5, 1, 2)
    best(1)
    lists("v", "n4u", 1)
    ids("v", "i4", twin, T.n4u, 512, IV, tall + ["n4u1"])
    ids("a", "i4", twin, T.n4u, IV, 1024, tall + ["n4u1"])
    value("i4", 6, 1, 3)
    best(2)
    V(["ps6", "b3"], ["res"], lambda: v.tensor_tensor(T.res[:], ps[6][:, 0:64], T.b3[:], A.max))

    half = [slice(64 * hi, 64 * hi + 64) for hi in range(2)]
    comp("t", ["res", "id"], ["ps7"], [lambda hi=hi: pe.matmul(ps[7][half[hi], 0:64], T.res[:], T["id"][:, hi:128:2], True, True) for hi in range(2)])
    p = ps[7][:, 0:64]
    V(["ps7"], ["rt"], lambda: v.tensor_scalar(T.rt[:], p, RND, RND, A.add, A.subtract))
    V(["ps7", "rt"], ["yi"], lambda: v.tensor_tensor(T.yi[:], p, T.rt[:], A.subtract))
    comp("a", ["rt"], ["yl"], lambda: g.scalar.activation(T.yl[:], T.rt[:], F.Copy, scale=1.0 / K17))
    for hi in range(2):
        dma("s", T.yid[:, 512 * hi:512 * hi + 512], T.yi[half[hi], :], ["yi"], ["oi%d" % hi])
        dma("a", T.ylen[:, 512 * hi:512 * hi + 512], T.yl[half[hi], :], ["yl"], ["ol%d" % hi])

    for s in total:
        if seen.get(s, 0) < total[s]:
            wait("g", [(s, total[s])])
